import numpy as np, ml_dtypes
CORES = [40,41,42,43,44,45,46,47]
N = 8
BF = ml_dtypes.bfloat16
def gentries(a):
    return np.ascontiguousarray(a.reshape(8, 16, -1).transpose(0, 2, 1)).reshape(8, -1)
def gtable(e):
    e = np.asarray(e); return np.ascontiguousarray(e.reshape(8, -1, 16).transpose(0, 2, 1)).reshape(128, -1).astype(np.int32)
P, S, C, R = 2048, 48, 64, 5
def members(v):
    return np.stack([gentries(u) for u in v]).reshape(N, 8, R, N, C)
def pack(x, w, a, b):
    w = np.repeat(w[:1], N, 0)
    return {"fld": x.reshape(N, 128, P).astype(np.float32).astype(BF), "law": w.reshape(N, 128, S * S).astype(np.float32).astype(BF),
            "la": np.stack([gtable(u.reshape(8, -1)) for u in a]), "lb": np.stack([gtable(u.reshape(8, -1)) for u in b])}
def cut(p):
    return p[..., :N * C].reshape(N, 8, R, N, C), p[..., N * C:2 * N * C].reshape(N, 8, R, N, C)
def raw(rng):
    x = rng.integers(-128, 129, (N, 8, 16, P)); x[:, :, 0] = rng.integers(0, S, (N, 8, P))
    w = rng.integers(-16, 17, (N, 8, 16, S * S)); w[:, :, :2] = rng.integers(0, S, (N, 8, 2, S * S))
    a, b = cut(rng.permuted(np.tile(np.arange(P), (N, 8, R, 1)), axis=-1))
    return x, w, a, b
def setup_inputs(rng):
    return pack(*raw(rng))
def setup_inputs_swap(rng):
    x, w, a, b = raw(rng); a2, b2 = a.copy(), b.copy()
    for t in range(R):
        a2[:, :, t], b2[:, :, t] = (a[:, :, 0], b[:, :, 0]) if t % 2 == 0 else (b[:, :, 0], a[:, :, 0])
    return pack(x, w, a2, b2)
def setup_inputs_ends(rng):
    x, w, a, b = raw(rng); x[:, :, 0] = (S - 1) * rng.integers(0, 2, (N, 8, P)); w[:, :, :2] = (S - 1) * rng.integers(0, 2, (N, 8, 2, S * S))
    x[:, :, 1:] = 256 * rng.integers(0, 2, (N, 8, 15, P)) - 128; w[:, :, 2:] = 32 * rng.integers(0, 2, (N, 8, 14, S * S)) - 16
    w[:, :, 2::2] = 32 * rng.integers(0, 2, (N, 8, 7, 1)) - 16
    p = np.concatenate([np.arange(N * C), np.arange(P)[::-1][:N * C]])
    a, b = cut(np.tile(p, (N, 8, R, 1))); return pack(x, w, a, b)
def setup_inputs_one(rng):
    x, w, a, b = raw(rng); x[:, :, 0] = rng.integers(0, S, (N, 8, 1)); return pack(x, w, a, b)
def setup_inputs_spread(rng):
    x, w, a, b = raw(rng)
    x[:, :, 0] = np.floor(S * rng.random((N, 8, P)) ** 3); w[:, :, :2] = np.floor(S * rng.random((N, 8, 2, S * S)) ** 3)
    x[:, :, 1:] = np.floor(np.exp2(7 * rng.random((N, 8, 15, P)))) * rng.choice(np.array([-1, 0, 1]), (N, 8, 15, P))
    w[:, :, 2:] = np.floor(np.exp2(4 * rng.random((N, 8, 14, S * S)))) * rng.choice(np.array([-1, 0, 0, 1]), (N, 8, 14, S * S))
    a, b = cut(np.argsort(rng.random((N, 8, R, P)) + 2 * rng.random((N, 8, 1, P)), axis=-1)); return pack(x, w, a, b)
def check_inputs(d):
    bad = []; x = np.asarray(d["fld"]).astype(np.float32).reshape(N, 8, 16, P); w = np.asarray(d["law"]).astype(np.float32).reshape(N, 8, 16, S * S)
    if not ((x == np.floor(x)).all() and (x[:, :, 0] >= 0).all() and (x[:, :, 0] < S).all() and (np.abs(x[:, :, 1:]) <= 128).all()): bad.append("fields")
    if not ((w == np.floor(w)).all() and (w[:, :, :2] >= 0).all() and (w[:, :, :2] < S).all() and (np.abs(w[:, :, 2:]) <= 16).all()): bad.append("law")
    if not (w == w[:1]).all(): bad.append("common")
    e = np.sort(np.concatenate([members(d["la"]).reshape(N, 8, R, N * C), members(d["lb"]).reshape(N, 8, R, N * C)], -1), -1)
    if not ((e >= 0).all() and (e < P).all()): bad.append("range")
    if not (e[..., 1:] > e[..., :-1]).all(): bad.append("disjoint")
    return bad
def reference(fld, law, la, lb):
    x = fld.astype(np.float32).astype(np.int64).reshape(N, 8, 16, P); w = law.astype(np.float32).astype(np.int64).reshape(N, 8, 16, S * S)
    a, b = members(la), members(lb)
    for t in range(R):
        for r in range(N):
            for q in range(N):
                for g in range(8):
                    u, v = x[r, g], x[q, g]; i, j = a[r, g, t, q], b[q, g, t, r]
                    col = w[r, g][:, u[0, i] * S + v[0, j]]
                    u[0, i] = col[0]; v[0, j] = col[1]
                    u[2:, i] += col[2:]; v[2:, j] -= col[2:]
    return {"y": x.reshape(N, 128, P).astype(np.float32)}

@@ -1,0 +1,265 @@
+from concourse.bass import DstId, RemoteDMATransfer
+from concourse.mybir import AluOpType as A, ActivationFunctionType as F
+
+N, P, S, R = 8, 2048, 48, 5
+K = 1024
+L = S * S
+HIST = 8192
+MID = 6144
+
+CFG = {"sc_a": [0, 512, 512, 512, 512], "pg": [0, 0, 0, 0, 0], "pt": [1, 1, 1, 1, 1], "split": 1, "wz": 128, "wv": 640,
+       "p1": 512, "fin": [256, 768, 1024]}
+
+SCRATCH = {
+    "la3": ("sbuf", [128, R, 32], "int32"), "lb3": ("sbuf", [128, R, 32], "int32"),
+    "lf": ("sbuf", [128, R, 64], "float32"), "lst": ("sbuf", [128, R * 64], "uint16"),
+    "hist": ("sbuf", [128, HIST], "bfloat16"), "laws": ("sbuf", [128, 2 * L], "bfloat16"),
+    "where": ("sbuf", [128, P], "float32"), "pos": ("sbuf", [128, R * K], "float32"),
+    "xs": ("sbuf", [128, R * K], "bfloat16"), "xm": ("sbuf", [128, R * K], "bfloat16"),
+    "p16": ("sbuf", [128, (R - 1) * K + P], "float16"),
+    "ptf": ("sbuf", [128, (R - 1) * 64 + 128], "float32"), "ptr": ("sbuf", [128, (R - 1) * 64 + 128], "uint16"),
+    "out": ("sbuf", [128, R * 64], "bfloat16"), "land": ("sbuf", [128, R * 64], "bfloat16"),
+    "own": ("sbuf", [128, R * 64], "float32"), "colf": ("sbuf", [128, R * 64], "float32"),
+    "col": ("sbuf", [128, R * 64], "uint16"),
+    "wts": ("sbuf", [128, 64], "bfloat16"), "offs": ("sbuf", [128, 64], "bfloat16"),
+    "pidx": ("sbuf", [128, 1], "int32"), "pm": ("sbuf", [128, 1], "int32"), "cst": ("sbuf", [128, 4], "float32"),
+    "diag": ("sbuf", [128, 144], "float32"), "eb": ("sbuf", [128, 144], "bfloat16"), "eh": ("sbuf", [128, 144], "float16"),
+    "num0": ("sbuf", [128, 128], "float32"), "num": ("sbuf", [128, 128], "float32"),
+    "kind": ("sbuf", [128, P], "bfloat16"), "res": ("sbuf", [128, P], "float32"),
+    "psa0": ("psum", [128, 512], "float32"), "psa1": ("psum", [128, 512], "float32"),
+    "psp0": ("psum", [128, 512], "float32"), "psp1": ("psum", [128, 512], "float32"),
+    "psf0": ("psum", [128, 512], "float32"), "psf1": ("psum", [128, 512], "float32"),
+}
+SEMAPHORES = ["arr%d_%d" % (t, i) for t in range(R) for i in range(2)] + ["sent"] + ["e%d" % i for i in range(139)]
+
+
+def region(t):
+    if t == 0:
+        return P, 2, 2 * P
+    return 2 * P + (t - 1) * K, 1, 2 * P + t * K
+
+
+def rank_program(g, core, T, topo):
+    me = T.rank_of(core)
+    if me is None:
+        return
+    V, SC, PE, Q = g.vector, g.scalar, g.tensor, g.sync
+    made, waited = [], {}
+
+    def ev(calls, n=1):
+        name = "e%d" % len(made)
+        for c in calls:
+            c.then_inc(T.sem[name], n)
+        made.append((name, n * len(calls)))
+        return made[-1]
+
+    def wait(q, *events):
+        for e in events:
+            q.wait_ge(T.sem[e[0]], e[1])
+            waited[e[0]] = 1
+
+    def to_list(ps, eye, src, c0, n):
+        last = None
+        for m in range(16):
+            last = PE.matmul(ps[:, 0:n], eye[:, 16 - m:144 - m], src[:, c0 + m:c0 + 16 * n:16], m == 0, m == 15)
+        return ev([last])
+
+    def iota(out, step, n, base, mult):
+        return ev([g.iota(out, [[step, n]], base, mult, allow_small_or_imprecise_dtypes=True)])
+
+    def positions(t, a, b):
+        c0, step, _ = region(t)
+        return iota(T.pos[:, t * K + a:t * K + b], step, b - a, c0 + step * a, 0)
+
+    wz, wv, p1 = CFG["wz"], CFG["wv"], CFG["p1"]
+    e_la = ev([Q.dma_start(T.la3[:], T.la[:])], 16)
+    e_lb = ev([SC.dma_start(T.lb3[:], T.lb[:])], 16)
+    e_w0 = ev([V.memset(T.where[:, 0:wz], 0.0)])
+    e_sp0 = ev([V.memset(T.kind[:], 0.0)])
+    wait(Q, e_sp0)
+    e_sp = ev([Q.dma_start(T.kind[0:128:16, :], T.fld[0:128:16, :])], 16)
+    e_law = ev([Q.dma_start(T.laws[:, 0:L], T.law[:])], 16)
+    e_fld = ev([Q.dma_start(T.hist[:, 0:P], T.fld[:])], 16)
+
+    e_p = ev([g.iota(T.pidx[:], [[0, 1]], 0, 1)])
+    e_diag = iota(T.diag[:], 1, 144, -16, -1)
+    e_pos = {0: positions(0, 0, K)}
+    e_pos1 = positions(1, 0, p1)
+    e_w1 = ev([V.memset(T.where[:, wz:wv], 0.0)])
+    wait(SC, e_w0)
+    e_w2 = ev([SC.activation(T.where[:, c:c + wz], T.where[:, 0:wz], F.Silu) for c in range(wv, P, wz)])
+    wait(V, e_p)
+    e_pm = ev([V.tensor_scalar(T.pm[:], T.pidx[:], 15, None, A.bitwise_and)])
+    lo = 8 * me
+    pieces = [(T.wts[:, lo:64:2], 48.0), (T.wts[:, lo + 1:64:2], 1.0)]
+    if me:
+        pieces += [(T.wts[:, 1:lo:2], 48.0), (T.wts[:, 0:lo:2], 1.0)]
+    e_wts = ev([V.memset(ap, x) for ap, x in pieces])
+    wait(V, e_pm)
+    row0, keep, sign, pmf = (T.cst[:, i:i + 1] for i in range(4))
+    e_cst = ev([V.tensor_scalar(row0, T.pm[:], 0.0, None, A.is_equal),
+                V.tensor_scalar(keep, T.pm[:], 0.0, None, A.not_equal),
+                V.tensor_scalar(sign, T.pm[:], 2.0, -1.0, A.is_ge, A.mult),
+                V.tensor_copy(pmf, T.pm[:])])
+    wait(V, e_diag, e_cst)
+    e_eb = ev([V.tensor_scalar(T.eb[:], T.diag[:], 0.0, row0, A.is_equal, A.mult)])
+
+    wait(V, e_la, e_lb)
+    h = 4 * me
+    moves = [(T.lf[:, :, lo:64:2], T.la3[:, :, h:32]), (T.lf[:, :, lo + 1:64:2], T.lb3[:, :, h:32])]
+    if me:
+        moves += [(T.lf[:, :, 1:lo:2], T.la3[:, :, 0:h]), (T.lf[:, :, 0:lo:2], T.lb3[:, :, 0:h])]
+    e_lf = ev([V.tensor_scalar(o, i, -float(MID), None, A.add) for o, i in moves])
+    wait(V, e_lf)
+    e_lst0 = ev([V.tensor_scalar(T.lst[:, 0:64], T.lf[:, 0, :], float(MID), None, A.add)])
+
+    def scatter(t, a, b):
+        return ev([SC.activation(T.where[:].indirect(T.lst[:, t * 64 + a // 16:t * 64 + b // 16]),
+                                 T.pos[:, t * K + a:t * K + b], F.Silu)])
+
+    far = [d for d in range(N) if topo.die(T.cores[d]) != topo.die(core)]
+    near = [d for d in range(N) if d not in far]
+    halves = [far, near] if CFG["split"] else [list(range(N))]
+    eng = topo.engines(core, T.cores[far[0]])
+    order = eng[0::2] + eng[1::2]
+    share = len(eng) // len(halves[0])
+    masks = {}
+    for part in halves:
+        peers = [d for d in far + near if d in part and d != me]
+        for i, d in enumerate(peers):
+            mine = eng[share * i:share * (i + 1)] if CFG["split"] else order[share * i:share * (i + 1)]
+            masks[d] = sum(1 << e for e in mine)
+    spans = [(8 * part[0], 8 * part[-1] + 8) for part in halves]
+
+    def pointers(e_mm, ps, like, c0):
+        wait(V, e_mm)
+        e = ev([V.tensor_tensor(T.ptf[:, c0:c0 + 64], ps[:, 0:64], like, A.max)])
+        wait(V, e)
+        return ev([V.tensor_scalar(T.ptr[:, c0:c0 + 64], T.ptf[:, c0:c0 + 64], MID + 0.25, None, A.add)])
+
+    ready, e_sa = [e_sp, e_lst0], None
+    for t in range(R):
+        b, c = t * K, t * 64
+        off, o0 = (T.ptr, c - 64) if t else (T.lst, 0)
+        win = T.hist[:, 0:region(t - 1)[2]] if t else T.kind[:]
+        wait(V, *ready)
+        wait(SC, *ready)
+        e_x, e_mm, e_out = [], [], []
+        for u0, u1 in spans:
+            um = (u0 + u1) // 2
+            e_x.append(ev([V.tensor_copy(T.xs[:, b + 16 * u0:b + 16 * um], win.indirect(off[:, o0 + u0:o0 + um])),
+                           SC.activation(T.xs[:, b + 16 * um:b + 16 * u1], win.indirect(off[:, o0 + um:o0 + u1]), F.Copy)]))
+        if t == 0:
+            wait(PE, e_eb)
+        for i, (u0, u1) in enumerate(spans):
+            wait(PE, e_x[i])
+            e_mm.append(to_list(T["psa%d" % i], T.eb, T.xs, b + 16 * u0, u1 - u0))
+        for i, (u0, u1) in enumerate(spans):
+            if t == 0 and i == 0:
+                wait(V, e_wts)
+                e_offs = ev([V.tensor_scalar(T.offs[:], T.wts[:], 1.0, float(L), A.is_equal, A.mult)])
+                e_eh = ev([V.tensor_scalar(T.eh[:], T.diag[:], 0.0, row0, A.is_equal, A.mult)])
+            if t == 0 and i == len(spans) - 1:
+                e_lst = ev([V.tensor_scalar(T.lst[:, 64:R * 64], T.lf[:, 1:R, :], float(MID), None, A.add)])
+            wait(V, e_mm[i])
+            e_out.append(ev([V.tensor_tensor(T.out[:, c + u0:c + u1], T["psa%d" % i][:, 0:u1 - u0], T.wts[:, u0:u1], A.mult)]))
+            wait(g, e_out[i])
+            transfers = []
+            for d in halves[i]:
+                if d != me:
+                    rid, pid, _ = topo.addr(T.cores[d])
+                    transfers.append(RemoteDMATransfer(dst_ids=[DstId(rid=rid, pnc=pid)], dma_engine_mask=masks[d],
+                                                       remote_sem=T.sem["arr%d_%d" % (t, i)], src=T.out[:, c + 8 * d:c + 8 * d + 8],
+                                                       dst=T.land[:, c + lo:c + lo + 8]))
+            g.remote_dma_fused(transfers, local_sem=T.sem.sent)
+        if t + 1 < R:
+            e_pos[t + 1] = positions(t + 1, 0 if t else p1, K)
+        if t == 0:
+            e_num0 = iota(T.num0[:], 16, 128, -MID, 0)
+
+        sa = CFG["sc_a"][t]
+        if t:
+            wait(SC, e_sa, e_pos[t])
+        else:
+            wait(SC, e_pos[0], e_w1, e_w2)
+        e_sb = scatter(t, sa, K)
+
+        if t == 0:
+            e_gap = ev([V.memset(T.hist[:, P + 1:2 * P:2], 0.0)])
+            wait(V, e_offs)
+        wait(V, *e_out)
+        e_own = ev([V.tensor_tensor(T.own[:, c:c + 64], T.out[:, c:c + 64], T.offs[:], A.add),
+                    V.tensor_copy(T.land[:, c + lo:c + lo + 8:2], T.out[:, c + lo + 1:c + lo + 8:2]),
+                    V.tensor_copy(T.land[:, c + lo + 1:c + lo + 8:2], T.out[:, c + lo:c + lo + 8:2])])
+        if t == 0:
+            wait(V, e_law)
+            e_l2 = ev([V.tensor_scalar(T.laws[:, L:2 * L], T.laws[:, 0:L], sign, None, A.mult)])
+            wait(Q, e_l2)
+            e_fix = ev([Q.dma_start(T.laws[0:128:16, L:2 * L], T.law[1:128:16, :]),
+                        Q.dma_start(T.laws[1:128:16, 0:L], T.laws[1:128:16, L:2 * L])], 16)
+            wait(V, e_fld)
+            e_xm = ev([V.tensor_scalar(T.xm[:, b:b + K], T.hist[:, 0:P].indirect(T.lst[:, 0:64]), keep, None, A.mult)])
+        else:
+            wait(V, *e_x)
+            e_xm = ev([V.tensor_scalar(T.xm[:, b:b + K], T.xs[:, b:b + K], keep, None, A.mult)])
+        if t == 1:
+            wait(V, e_num0)
+            e_num = ev([V.tensor_scalar(T.num[:], T.num0[:], pmf, None, A.add)])
+        jobs, ready = [], []
+
+        def newest():
+            wait(V, e_sb)
+            if t == 0:
+                wait(V, e_lst)
+                wait(PE, e_eh)
+            if t + 1 < R:
+                e_pg = ev([V.tensor_scalar(T.p16[:, b:b + K], T.where[:].indirect(T.lst[:, c + 64:c + 128]), -float(MID), None, A.add)])
+                wait(PE, e_pg)
+                jobs.append((to_list(T["psp%d" % (t % 2)], T.eh, T.p16, b, 64), T["psp%d" % (t % 2)], T.lf[:, t + 1, :], c))
+                wait(SC, e_pg)
+                wait(SC, *([e_pos[t + 1]] if t else [e_lst, e_pos1]))
+                return scatter(t + 1, 0, CFG["sc_a"][t + 1])
+            for u in range(2):
+                e_pg = ev([V.tensor_scalar(T.p16[:, b + u * K:b + u * K + K], T.where[:, u * K:u * K + K], -float(MID), None, A.add)])
+                wait(PE, e_pg)
+                jobs.append((to_list(T["psf%d" % u], T.eh, T.p16, b + u * K, 64), T["psf%d" % u], T.num[:, 64 * u:64 * u + 64], c + 64 * u))
+            wait(V, e_num)
+            return None
+
+        c0, step, _ = region(t)
+        for i in range(len(spans) + 1):
+            if i == min(CFG["pg"][t], len(spans)):
+                e_sa = newest()
+            if i == min(CFG["pt"][t], len(spans)):
+                ready += [pointers(*j) for j in jobs]
+            if i == len(spans):
+                break
+            u0, u1 = spans[i]
+            V.wait_ge(T.sem["arr%d_%d" % (t, i)], share * len([d for d in halves[i] if d != me]))
+            if i == 0:
+                wait(V, e_own)
+            e_add = ev([V.tensor_tensor(T.colf[:, c + u0:c + u1], T.own[:, c + u0:c + u1], T.land[:, c + u0:c + u1], A.add)])
+            wait(V, e_add)
+            e_col = ev([V.tensor_copy(T.col[:, c + u0:c + u1], T.colf[:, c + u0:c + u1])])
+            wait(V, e_col)
+            if i == 0:
+                wait(V, e_xm)
+                if t == 0:
+                    wait(V, e_fix, e_gap)
+            ready.append(ev([V.tensor_tensor(T.hist[:, c0 + step * 16 * u0:c0 + step * 16 * u1:step], T.laws[:].indirect(T.col[:, c + u0:c + u1]),
+                                             T.xm[:, b + 16 * u0:b + 16 * u1], A.add)]))
+
+    f0 = (R - 1) * 64
+    wait(V, *ready)
+    wait(SC, *ready)
+    stores, c0 = [], 0
+    for n in CFG["fin"]:
+        cm, c1 = c0 + n // 2, c0 + n
+        e = ev([V.tensor_copy(T.res[:, c0:cm], T.hist[:].indirect(T.ptr[:, f0 + c0 // 16:f0 + cm // 16])),
+                SC.activation(T.res[:, cm:c1], T.hist[:].indirect(T.ptr[:, f0 + cm // 16:f0 + c1 // 16]), F.Copy)])
+        wait(Q, e)
+        stores.append(Q.dma_start(T.y[:, c0:c1], T.res[:, c0:c1]))
+        c0 = c1
+    wait(Q, ev(stores, 16))
+    g.wait_ge(T.sem.sent, share * (N - 1) * R)
+    wait(g, *[e for e in made if e[0] not in waited])

@@ -3,40 +3,37 @@ from concourse.mybir import AluOpType as A, ActivationFunctionType as F
 
 N, P, S, R = 8, 2048, 48, 5
 K = 1024
+H = K // 2
 L = S * S
-HIST = 8192
-MID = 6144
+HIST = P + R * K
+RADIX = 32
 
-CFG = {"sc_a": [0, 512, 512, 512, 512], "pg": [0, 0, 0, 0, 0], "pt": [1, 1, 1, 1, 1], "split": 1, "wz": 128, "wv": 640,
-       "p1": 512, "fin": [256, 768, 1024]}
+CFG = {"late": 0, "gf": [20, 20, 20, 20, 20], "gn": [24, 24, 24, 24, 24], "pgv": [32, 32, 32, 32], "sa": [512, 512, 512, 512, 512],
+       "pg": [0, 0, 0, 0, 0], "pm": [1, 1, 1, 1, 1], "pt": [2, 2, 2, 2, 2], "wz": 256, "wv": 0, "wl": 0, "ws": 512, "cv": 512, "x0": 32,
+       "fin": [256, 768, 1024], "fv": 0.5, "near": [3], "dg": 0, "tb": 1, "pk": 1, "p11": -1, "l0": 768}
 
 SCRATCH = {
     "la3": ("sbuf", [128, R, 32], "int32"), "lb3": ("sbuf", [128, R, 32], "int32"),
-    "lf": ("sbuf", [128, R, 64], "float32"), "lst": ("sbuf", [128, R * 64], "uint16"),
+    "lst": ("sbuf", [128, R, 64], "uint16"), "lf": ("sbuf", [128, R, 64], "float32"),
     "hist": ("sbuf", [128, HIST], "bfloat16"), "laws": ("sbuf", [128, 2 * L], "bfloat16"),
-    "where": ("sbuf", [128, P], "float32"), "pos": ("sbuf", [128, R * K], "float32"),
-    "xs": ("sbuf", [128, R * K], "bfloat16"), "xm": ("sbuf", [128, R * K], "bfloat16"),
-    "p16": ("sbuf", [128, (R - 1) * K + P], "float16"),
+    "where": ("sbuf", [128, P], "float32"), "pos": ("sbuf", [128, (R - 1) * K], "float32"),
+    "hi": ("sbuf", [128, 4 * RADIX], "float32"),
+    "xs": ("sbuf", [128, R * K], "bfloat16"), "x0": ("sbuf", [128, K], "bfloat16"),
+    "pd": ("sbuf", [128, (R - 1) * K + P], "bfloat16"),
     "ptf": ("sbuf", [128, (R - 1) * 64 + 128], "float32"), "ptr": ("sbuf", [128, (R - 1) * 64 + 128], "uint16"),
     "out": ("sbuf", [128, R * 64], "bfloat16"), "land": ("sbuf", [128, R * 64], "bfloat16"),
-    "own": ("sbuf", [128, R * 64], "float32"), "colf": ("sbuf", [128, R * 64], "float32"),
-    "col": ("sbuf", [128, R * 64], "uint16"),
-    "wts": ("sbuf", [128, 64], "bfloat16"), "offs": ("sbuf", [128, 64], "bfloat16"),
-    "pidx": ("sbuf", [128, 1], "int32"), "pm": ("sbuf", [128, 1], "int32"), "cst": ("sbuf", [128, 4], "float32"),
-    "diag": ("sbuf", [128, 144], "float32"), "eb": ("sbuf", [128, 144], "bfloat16"), "eh": ("sbuf", [128, 144], "float16"),
+    "col": ("sbuf", [128, R * 64], "uint16"), "offs": ("sbuf", [128, 32], "bfloat16"),
+    "pidx": ("sbuf", [128, 1], "int32"), "pm": ("sbuf", [128, 1], "int32"), "cst": ("sbuf", [128, 8], "float32"),
+    "diag": ("sbuf", [128, 144], "float32"), "eb": ("sbuf", [128, 144], "bfloat16"), "ed": ("sbuf", [128, 144], "bfloat16"),
+    "one": ("sbuf", [128, 128], "bfloat16"), "big": ("sbuf", [128, 128], "bfloat16"),
     "num0": ("sbuf", [128, 128], "float32"), "num": ("sbuf", [128, 128], "float32"),
     "kind": ("sbuf", [128, P], "bfloat16"), "res": ("sbuf", [128, P], "float32"),
     "psa0": ("psum", [128, 512], "float32"), "psa1": ("psum", [128, 512], "float32"),
+    "psc0": ("psum", [128, 512], "float32"), "psc1": ("psum", [128, 512], "float32"),
+    "psc2": ("psum", [128, 512], "float32"), "psc3": ("psum", [128, 512], "float32"),
     "psp0": ("psum", [128, 512], "float32"), "psp1": ("psum", [128, 512], "float32"),
-    "psf0": ("psum", [128, 512], "float32"), "psf1": ("psum", [128, 512], "float32"),
 }
-SEMAPHORES = ["arr%d_%d" % (t, i) for t in range(R) for i in range(2)] + ["sent"] + ["e%d" % i for i in range(139)]
-
-
-def region(t):
-    if t == 0:
-        return P, 2, 2 * P
-    return 2 * P + (t - 1) * K, 1, 2 * P + t * K
+SEMAPHORES = ["arr%d_%d" % (t, i) for t in range(R) for i in range(3)] + ["sent", "vv"] + ["e%d" % i for i in range(133)]
 
 
 def rank_program(g, core, T, topo):
@@ -44,7 +41,7 @@ def rank_program(g, core, T, topo):
     if me is None:
         return
     V, SC, PE, Q = g.vector, g.scalar, g.tensor, g.sync
-    made, waited = [], {}
+    made, waited, steps = [], {}, [0]
 
     def ev(calls, n=1):
         name = "e%d" % len(made)
@@ -58,208 +55,335 @@ def rank_program(g, core, T, topo):
             q.wait_ge(T.sem[e[0]], e[1])
             waited[e[0]] = 1
 
+    def step(*calls):
+        for c in calls:
+            c.then_inc(T.sem.vv, 1)
+        steps[0] += len(calls)
+        V.wait_ge(T.sem.vv, steps[0])
+
     def to_list(ps, eye, src, c0, n):
         last = None
         for m in range(16):
             last = PE.matmul(ps[:, 0:n], eye[:, 16 - m:144 - m], src[:, c0 + m:c0 + 16 * n:16], m == 0, m == 15)
         return ev([last])
 
-    def iota(out, step, n, base, mult):
-        return ev([g.iota(out, [[step, n]], base, mult, allow_small_or_imprecise_dtypes=True)])
+    def iota(out, pattern, base, mult):
+        return ev([g.iota(out, pattern, base, mult, allow_small_or_imprecise_dtypes=True)])
 
-    def positions(t, a, b):
-        c0, step, _ = region(t)
-        return iota(T.pos[:, t * K + a:t * K + b], step, b - a, c0 + step * a, 0)
+    def shared(out, o0, win, off, u0, um, u1):
+        calls = []
+        if um > u0:
+            calls.append(V.tensor_copy(out[:, o0:o0 + 16 * (um - u0)], win.indirect(off(u0, um))))
+        if u1 > um:
+            calls.append(SC.activation(out[:, o0 + 16 * (um - u0):o0 + 16 * (u1 - u0)], win.indirect(off(um, u1)), F.Copy))
+        return ev(calls)
 
-    wz, wv, p1 = CFG["wz"], CFG["wv"], CFG["p1"]
-    e_la = ev([Q.dma_start(T.la3[:], T.la[:])], 16)
-    e_lb = ev([SC.dma_start(T.lb3[:], T.lb[:])], 16)
+    def blocks(r):
+        same = [d for d in range(N) if topo.die(T.cores[d]) == topo.die(T.cores[r])]
+        i = same.index(r) + 1
+        return same[i:] + same[:i] + [d for d in range(N) if d not in same]
+
+    order = blocks(me)
+    own = order.index(me)
+    eng = topo.engines(core, T.cores[order[-1]])
+    parts, k0 = [(own + 1, N)], 0
+    for n in CFG["near"]:
+        parts.append((k0, k0 + n))
+        k0 += n
+    share = [len(eng) // (1 << (k1 - k0 - 1).bit_length()) for k0, k1 in parts]
+
+    late, wz, l0 = CFG["late"], CFG["wz"], CFG["l0"]
+    wv = wz + CFG["wv"]
+    wl = wv + CFG["wl"]
+    ws = wl + CFG["ws"]
+    e_la = ev([Q.dma_start(T.la3[:], T.la[:]), SC.dma_start(T.lb3[:], T.lb[:])], 16)
+    early = [Q.dma_start(T.laws[:, 0:l0], T.law[:, 0:l0])] if l0 else []
     e_w0 = ev([V.memset(T.where[:, 0:wz], 0.0)])
-    e_sp0 = ev([V.memset(T.kind[:], 0.0)])
+    first = T.hist if late else T.kind
+    e_sp0 = ev([V.memset(first[:, 0:P], 0.0)])
     wait(Q, e_sp0)
-    e_sp = ev([Q.dma_start(T.kind[0:128:16, :], T.fld[0:128:16, :])], 16)
-    e_law = ev([Q.dma_start(T.laws[:, 0:L], T.law[:])], 16)
-    e_fld = ev([Q.dma_start(T.hist[:, 0:P], T.fld[:])], 16)
+    e_sp = ev([Q.dma_start(first[0:128:16, 0:P], T.fld[0:128:16, :])], 16)
+    e_fl = []
 
+    def law():
+        return ev(early + [Q.dma_start(T.laws[:, l0:L], T.law[:, l0:L])], 16)
+
+    if CFG["pk"] == 0:
+        e_law = law()
+
+    low = [[0, H // RADIX], [1, RADIX]]
     e_p = ev([g.iota(T.pidx[:], [[0, 1]], 0, 1)])
-    e_diag = iota(T.diag[:], 1, 144, -16, -1)
-    e_pos = {0: positions(0, 0, K)}
-    e_pos1 = positions(1, 0, p1)
-    e_w1 = ev([V.memset(T.where[:, wz:wv], 0.0)])
+    if CFG["dg"]:
+        e_diag = iota(T.diag[:], [[1, 144]], -16, -1)
+    e_lo = [iota(T.pos[:, 0:H], low, RADIX, 0)]
+    if not CFG["dg"]:
+        e_diag = iota(T.diag[:], [[1, 144]], -16, -1)
+    e_lo.append(iota(T.pos[:, H:K], low, RADIX, 0))
     wait(SC, e_w0)
-    e_w2 = ev([SC.activation(T.where[:, c:c + wz], T.where[:, 0:wz], F.Silu) for c in range(wv, P, wz)])
-    wait(V, e_p)
-    e_pm = ev([V.tensor_scalar(T.pm[:], T.pidx[:], 15, None, A.bitwise_and)])
-    lo = 8 * me
-    pieces = [(T.wts[:, lo:64:2], 48.0), (T.wts[:, lo + 1:64:2], 1.0)]
-    if me:
-        pieces += [(T.wts[:, 1:lo:2], 48.0), (T.wts[:, 0:lo:2], 1.0)]
-    e_wts = ev([V.memset(ap, x) for ap, x in pieces])
-    wait(V, e_pm)
-    row0, keep, sign, pmf = (T.cst[:, i:i + 1] for i in range(4))
-    e_cst = ev([V.tensor_scalar(row0, T.pm[:], 0.0, None, A.is_equal),
-                V.tensor_scalar(keep, T.pm[:], 0.0, None, A.not_equal),
-                V.tensor_scalar(sign, T.pm[:], 2.0, -1.0, A.is_ge, A.mult),
-                V.tensor_copy(pmf, T.pm[:])])
-    wait(V, e_diag, e_cst)
-    e_eb = ev([V.tensor_scalar(T.eb[:], T.diag[:], 0.0, row0, A.is_equal, A.mult)])
 
-    wait(V, e_la, e_lb)
-    h = 4 * me
-    moves = [(T.lf[:, :, lo:64:2], T.la3[:, :, h:32]), (T.lf[:, :, lo + 1:64:2], T.lb3[:, :, h:32])]
-    if me:
-        moves += [(T.lf[:, :, 1:lo:2], T.la3[:, :, 0:h]), (T.lf[:, :, 0:lo:2], T.lb3[:, :, 0:h])]
-    e_lf = ev([V.tensor_scalar(o, i, -float(MID), None, A.add) for o, i in moves])
-    wait(V, e_lf)
-    e_lst0 = ev([V.tensor_scalar(T.lst[:, 0:64], T.lf[:, 0, :], float(MID), None, A.add)])
+    def zero(c0, c1):
+        return ev([SC.activation(T.where[:, c:min(c1, c + wz)], T.where[:, 0:min(wz, c1 - c)], F.Silu) for c in range(c0, c1, wz)])
+
+    e_w2 = zero(ws, P)
+    wait(V, e_p)
+    step(V.tensor_scalar(T.pm[:], T.pidx[:], 15, None, A.bitwise_and))
+    row0, sign, pmf, keep, neg, wt, wd = (T.cst[:, i:i + 1] for i in range(7))
+    step(V.tensor_copy(pmf, T.pm[:]), V.tensor_scalar(row0, T.pm[:], 0.0, None, A.is_equal))
+    wait(V, e_w0)
+
+    def high(t):
+        src, add = (T.hi[:, 0:RADIX], 0.0) if t else (T.where[:, 0:RADIX], pmf)
+        return ev([V.tensor_scalar(T.hi[:, RADIX * j:RADIX * (j + 1)], src, add, float(16 * j + (0 if t else P // RADIX)), A.add, A.add)
+                   for j in (2 * t, 2 * t + 1)])
+
+    def patch(t, h):
+        j = 2 * t + h
+        return ev([Q.dma_start(T.pos[0:128:16, h * H:h * H + H], T.hi[:, RADIX * j:RADIX * (j + 1)])], 16)
+
+    def eye():
+        wait(V, e_diag)
+        return ev([V.tensor_scalar(T.eb[:], T.diag[:], 0.0, row0, A.is_equal, A.mult)])
+
+    e_hi = {0: high(0)}
+    e_cst = ev([V.tensor_scalar(sign, T.pm[:], 2.0, -1.0, A.is_ge, A.mult)])
+    e_w1 = [ev([V.memset(T.where[:, wz:wv], 0.0)])] if wv > wz else []
+    if CFG["dg"]:
+        e_eb = eye()
+    wait(Q, e_hi[0], e_lo[0])
+    e_pos = {0: [patch(0, 0)]}
+    if CFG["pk"] == 1:
+        e_law = law()
+    wait(Q, e_lo[1])
+    e_pos[0].append(patch(0, 1))
+    if not late:
+        e_fld = ev([Q.dma_start(T.hist[:, 0:P], T.fld[:])], 16)
+
+    def moves(k0, k1):
+        calls = []
+        while k0 < k1:
+            k = k0 + 1
+            while k < k1 and order[k] == order[k - 1] + 1:
+                k += 1
+            d0, d1 = order[k0], order[k - 1] + 1
+            calls += [V.tensor_copy(T.lst[:, :, 8 * k0:8 * k:2], T.la3[:, :, 4 * d0:4 * d1]),
+                      V.tensor_copy(T.lst[:, :, 8 * k0 + 1:8 * k:2], T.lb3[:, :, 4 * d0:4 * d1])]
+            k0 = k
+        return ev(calls)
+
+    wait(V, e_la)
+    e_lst = moves(0, N)
+    if not CFG["dg"]:
+        e_eb = eye()
 
     def scatter(t, a, b):
-        return ev([SC.activation(T.where[:].indirect(T.lst[:, t * 64 + a // 16:t * 64 + b // 16]),
-                                 T.pos[:, t * K + a:t * K + b], F.Silu)])
+        c0 = max(t - 1, 0) * K
+        return ev([SC.activation(T.where[:].indirect(T.lst[:, t, a // 16:b // 16]), T.pos[:, c0 + a:c0 + b], F.Silu)])
 
-    far = [d for d in range(N) if topo.die(T.cores[d]) != topo.die(core)]
-    near = [d for d in range(N) if d not in far]
-    halves = [far, near] if CFG["split"] else [list(range(N))]
-    eng = topo.engines(core, T.cores[far[0]])
-    order = eng[0::2] + eng[1::2]
-    share = len(eng) // len(halves[0])
-    masks = {}
-    for part in halves:
-        peers = [d for d in far + near if d in part and d != me]
-        for i, d in enumerate(peers):
-            mine = eng[share * i:share * (i + 1)] if CFG["split"] else order[share * i:share * (i + 1)]
-            masks[d] = sum(1 << e for e in mine)
-    spans = [(8 * part[0], 8 * part[-1] + 8) for part in halves]
+    def tables():
+        wait(V, e_law, e_cst)
+        e = ev([V.tensor_scalar(T.laws[:, L:2 * L], T.laws[:, 0:L], sign, None, A.mult)])
+        wait(Q, e)
+        return ev([Q.dma_start(T.laws[0:128:16, L:2 * L], T.law[1:128:16, :]),
+                   Q.dma_start(T.laws[1:128:16, 0:L], T.laws[1:128:16, L:2 * L])], 16)
 
-    def pointers(e_mm, ps, like, c0):
-        wait(V, e_mm)
-        e = ev([V.tensor_tensor(T.ptf[:, c0:c0 + 64], ps[:, 0:64], like, A.max)])
-        wait(V, e)
-        return ev([V.tensor_scalar(T.ptr[:, c0:c0 + 64], T.ptf[:, c0:c0 + 64], MID + 0.25, None, A.add)])
-
-    ready, e_sa = [e_sp, e_lst0], None
+    spans = [(8 * own, 64), (0, 8 * own)]
+    ready, e_sa, e_sb = [e_sp, e_lst], None, None
     for t in range(R):
         b, c = t * K, t * 64
-        off, o0 = (T.ptr, c - 64) if t else (T.lst, 0)
-        win = T.hist[:, 0:region(t - 1)[2]] if t else T.kind[:]
+        if t:
+            win, off = T.hist[:, 0:P + t * K], lambda u0, u1: T.ptr[:, c - 64 + u0:c - 64 + u1]
+        else:
+            win, off = first[:, 0:P], lambda u0, u1: T.lst[:, 0, u0:u1]
+        if 0 < t < R - 1:
+            wait(Q, ready[-1], e_hi[t + 1])
+            e_pos[t + 1] = [ev([Q.dma_start(T.pos[1:128:16, t * K:(t + 1) * K], T.pos[1:128:16, 0:K])], 16)] * 2
+            if late and t < 3:
+                e_fl.append(Q.dma_start(T.kind[:, (t - 1) * K:t * K], T.fld[:, (t - 1) * K:t * K]))
+            if late and t == 3:
+                wait(Q, ev(e_fl, 16))
+                e_fld = ev([Q.dma_start(T.kind[0:128:16, :], T.hist[1:128:16, 0:P])], 16)
         wait(V, *ready)
         wait(SC, *ready)
-        e_x, e_mm, e_out = [], [], []
-        for u0, u1 in spans:
-            um = (u0 + u1) // 2
-            e_x.append(ev([V.tensor_copy(T.xs[:, b + 16 * u0:b + 16 * um], win.indirect(off[:, o0 + u0:o0 + um])),
-                           SC.activation(T.xs[:, b + 16 * um:b + 16 * u1], win.indirect(off[:, o0 + um:o0 + u1]), F.Copy)]))
+        e_x, e_mm, e_out, e_old = [], [], [], []
+        for i, (u0, u1) in enumerate(spans):
+            e_x.append(shared(T.xs, b + 16 * u0, win, off, u0, u0 + CFG["gn" if i else "gf"][t], u1))
         if t == 0:
             wait(PE, e_eb)
+            if ws > wl:
+                e_w1.append(zero(wl, ws))
+            if wl > wv:
+                e_w1.append(ev([V.memset(T.where[:, wv:wl], 0.0)]))
         for i, (u0, u1) in enumerate(spans):
             wait(PE, e_x[i])
             e_mm.append(to_list(T["psa%d" % i], T.eb, T.xs, b + 16 * u0, u1 - u0))
+            if t:
+                wait(Q, e_mm[i])
+                e_old.append(ev([Q.dma_start(T.xs[0:128:16, b + 16 * u0:b + 16 * u1], first[1:128:16, 16 * u0:16 * u1])], 16))
         for i, (u0, u1) in enumerate(spans):
-            if t == 0 and i == 0:
-                wait(V, e_wts)
-                e_offs = ev([V.tensor_scalar(T.offs[:], T.wts[:], 1.0, float(L), A.is_equal, A.mult)])
-                e_eh = ev([V.tensor_scalar(T.eh[:], T.diag[:], 0.0, row0, A.is_equal, A.mult)])
-            if t == 0 and i == len(spans) - 1:
-                e_lst = ev([V.tensor_scalar(T.lst[:, 64:R * 64], T.lf[:, 1:R, :], float(MID), None, A.add)])
+            if t == 0 and i == 1 and CFG["tb"]:
+                e_fix = tables()
+            if t == R - 1 and i == 1:
+                wait(V, e_num0)
+                e_num = ev([V.tensor_scalar(T.num[:], T.num0[:], pmf, None, A.add)])
             wait(V, e_mm[i])
-            e_out.append(ev([V.tensor_tensor(T.out[:, c + u0:c + u1], T["psa%d" % i][:, 0:u1 - u0], T.wts[:, u0:u1], A.mult)]))
+            e_out.append(ev([V.tensor_copy(T.out[:, c + u0:c + u1], T["psa%d" % i][:, 0:u1 - u0])]))
             wait(g, e_out[i])
-            transfers = []
-            for d in halves[i]:
-                if d != me:
+            for j in ([0] if i == 0 else range(1, len(parts))):
+                transfers = []
+                for n, k in enumerate(range(*parts[j])):
+                    d = order[k]
                     rid, pid, _ = topo.addr(T.cores[d])
-                    transfers.append(RemoteDMATransfer(dst_ids=[DstId(rid=rid, pnc=pid)], dma_engine_mask=masks[d],
-                                                       remote_sem=T.sem["arr%d_%d" % (t, i)], src=T.out[:, c + 8 * d:c + 8 * d + 8],
-                                                       dst=T.land[:, c + lo:c + lo + 8]))
-            g.remote_dma_fused(transfers, local_sem=T.sem.sent)
-        if t + 1 < R:
-            e_pos[t + 1] = positions(t + 1, 0 if t else p1, K)
-        if t == 0:
-            e_num0 = iota(T.num0[:], 16, 128, -MID, 0)
+                    at = c + 8 * blocks(d).index(me)
+                    transfers.append(RemoteDMATransfer(dst_ids=[DstId(rid=rid, pnc=pid)],
+                                                       dma_engine_mask=sum(1 << e for e in eng[share[j] * n:share[j] * (n + 1)]),
+                                                       remote_sem=T.sem["arr%d_%d" % (t, j)], src=T.out[:, c + 8 * k:c + 8 * k + 8],
+                                                       dst=T.land[:, at:at + 8]))
+                g.remote_dma_fused(transfers, local_sem=T.sem.sent)
+        if t + 2 < R:
+            e_hi[t + 2] = iota(T.pos[:, (t + 1) * K:(t + 2) * K], [[1, K // RADIX], [0, RADIX]], (P + (t + 2) * K) // RADIX, 0)
+        elif t + 2 == R:
+            e_num0 = iota(T.num0[:], [[16, 128]], RADIX, 0)
 
-        sa = CFG["sc_a"][t]
-        if t:
-            wait(SC, e_sa, e_pos[t])
-        else:
-            wait(SC, e_pos[0], e_w1, e_w2)
-        e_sb = scatter(t, sa, K)
+        sa = CFG["sa"][t]
+        if t == 0:
+            wait(SC, e_pos[0][0], e_w2, e_hi[0], *e_w1)
+            e_sa = scatter(0, 0, sa)
+        wait(SC, e_sa, *e_pos[t])
+        e_sb = scatter(t, sa, K) if sa < K else e_sa
+
+        def own_terms(ps, k0, k1):
+            n, a = 8 * (k1 - k0), c + 8 * k0
+            PE.matmul(ps[:, 0:n], T.one[:], T.offs[:, 0:n], True, False)
+            PE.matmul(ps[:, 0:n:2], T.big[:], T.out[:, a:a + n:2], False, False)
+            PE.matmul(ps[:, 1:n:2], T.one[:], T.out[:, a + 1:a + n:2], False, False)
+
+        def partner_terms(ps, src, k0, k1):
+            n, a = 8 * (k1 - k0), c + 8 * k0
+            PE.matmul(ps[:, 0:n:2], T.one[:], src[:, a + 1:a + n:2], False, False)
+            return ev([PE.matmul(ps[:, 1:n:2], T.big[:], src[:, a:a + n:2], False, True)])
 
         if t == 0:
-            e_gap = ev([V.memset(T.hist[:, P + 1:2 * P:2], 0.0)])
-            wait(V, e_offs)
-        wait(V, *e_out)
-        e_own = ev([V.tensor_tensor(T.own[:, c:c + 64], T.out[:, c:c + 64], T.offs[:], A.add),
-                    V.tensor_copy(T.land[:, c + lo:c + lo + 8:2], T.out[:, c + lo + 1:c + lo + 8:2]),
-                    V.tensor_copy(T.land[:, c + lo + 1:c + lo + 8:2], T.out[:, c + lo:c + lo + 8:2])])
+            if not CFG["tb"]:
+                e_fix = tables()
+            e_id = ev([V.tensor_scalar(T.one[:], T.diag[:, 16:144], 0.0, None, A.is_equal),
+                       V.tensor_scalar(T.big[:], T.diag[:, 16:144], 0.0, float(S), A.is_equal, A.mult),
+                       V.memset(T.offs[:, 0:32:2], 0.0), V.memset(T.offs[:, 1:32:2], float(L))])
+            wait(V, e_hi[0])
+            e_hi[1] = high(1)
+            wait(Q, e_hi[1], e_sa)
+            e_pos[1] = [patch(1, 0)]
+            wait(PE, e_id)
+        wait(PE, *e_out)
+        own_terms(T.psc0, own, own + 1)
+        e_sum = [partner_terms(T.psc0, T.out, own, own + 1)]
+        for j, part in enumerate(parts):
+            own_terms(T["psc%d" % (j + 1)], *part)
+
         if t == 0:
-            wait(V, e_law)
-            e_l2 = ev([V.tensor_scalar(T.laws[:, L:2 * L], T.laws[:, 0:L], sign, None, A.mult)])
-            wait(Q, e_l2)
-            e_fix = ev([Q.dma_start(T.laws[0:128:16, L:2 * L], T.law[1:128:16, :]),
-                        Q.dma_start(T.laws[1:128:16, 0:L], T.laws[1:128:16, L:2 * L])], 16)
-            wait(V, e_fld)
-            e_xm = ev([V.tensor_scalar(T.xm[:, b:b + K], T.hist[:, 0:P].indirect(T.lst[:, 0:64]), keep, None, A.mult)])
-        else:
-            wait(V, *e_x)
-            e_xm = ev([V.tensor_scalar(T.xm[:, b:b + K], T.xs[:, b:b + K], keep, None, A.mult)])
-        if t == 1:
-            wait(V, e_num0)
-            e_num = ev([V.tensor_scalar(T.num[:], T.num0[:], pmf, None, A.add)])
-        jobs, ready = [], []
+            step(V.tensor_scalar(neg, T.pm[:], -1.0, None, A.mult),
+                 V.tensor_scalar(keep, T.pm[:], 0.0, None, A.not_equal),
+                 V.tensor_scalar(wt, T.pm[:], 1.0 - RADIX, float(RADIX), A.mult, A.add))
+            step(V.tensor_scalar(wd, wt, 0.0, None, A.max))
+            e_ed = ev([V.tensor_scalar(T.ed[:], T.diag[:], neg, wd, A.is_equal, A.mult)])
+            e_lf = ev([V.tensor_scalar(T.lf[:, 1:R, :], T.lst[:, 1:R, :], float(RADIX), None, A.add)])
+            if not late:
+                wait(V, e_fld)
+                n0 = CFG["x0"]
+                e_old = [ev([V.tensor_scalar(T.x0[:, 0:16 * n0], T.hist[:, 0:P].indirect(off(0, n0)), keep, None, A.mult)])]
+        jobs, ready, tail = [], [], []
 
         def newest():
             wait(V, e_sb)
-            if t == 0:
-                wait(V, e_lst)
-                wait(PE, e_eh)
+            wait(SC, e_sb)
             if t + 1 < R:
-                e_pg = ev([V.tensor_scalar(T.p16[:, b:b + K], T.where[:].indirect(T.lst[:, c + 64:c + 128]), -float(MID), None, A.add)])
-                wait(PE, e_pg)
-                jobs.append((to_list(T["psp%d" % (t % 2)], T.eh, T.p16, b, 64), T["psp%d" % (t % 2)], T.lf[:, t + 1, :], c))
-                wait(SC, e_pg)
-                wait(SC, *([e_pos[t + 1]] if t else [e_lst, e_pos1]))
-                return scatter(t + 1, 0, CFG["sc_a"][t + 1])
+                e_pg = shared(T.pd, b, T.where[:], lambda u0, u1: T.lst[:, t + 1, u0:u1], 0, CFG["pgv"][t], 64)
+                jobs.append((e_pg, T["psp%d" % (t % 2)], b, T.lf[:, t + 1, :], c))
+                if t == 0 and not late and CFG["x0"] < 64:
+                    wait(SC, e_fld, e_ed)
+                    e_old.append(ev([SC.activation(T.x0[:, 16 * n0:K], T.hist[:, 0:P].indirect(off(n0, 64)), F.Copy, scale=keep)]))
+                n = CFG["sa"][t + 1]
+                if n == 0:
+                    return e_pg
+                wait(SC, e_pg, e_pos[t + 1][0])
+                return scatter(t + 1, 0, n)
+            cv = CFG["cv"]
             for u in range(2):
-                e_pg = ev([V.tensor_scalar(T.p16[:, b + u * K:b + u * K + K], T.where[:, u * K:u * K + K], -float(MID), None, A.add)])
-                wait(PE, e_pg)
-                jobs.append((to_list(T["psf%d" % u], T.eh, T.p16, b + u * K, 64), T["psf%d" % u], T.num[:, 64 * u:64 * u + 64], c + 64 * u))
-            wait(V, e_num)
+                a = u * K
+                calls = [V.tensor_copy(T.pd[:, b + a:b + a + cv], T.where[:, a:a + cv])]
+                if cv < K:
+                    calls.append(SC.activation(T.pd[:, b + a + cv:b + a + K], T.where[:, a + cv:a + K], F.Copy))
+                jobs.append((ev(calls), T["psp%d" % u], b + a, T.num[:, 64 * u:64 * u + 64], c + 64 * u))
             return None
 
-        c0, step, _ = region(t)
-        for i in range(len(spans) + 1):
-            if i == min(CFG["pg"][t], len(spans)):
+        todo = list(range(len(parts)))
+        todo.insert(min(CFG["pm"][t], len(parts)), "list")
+
+        def tensor_until(item):
+            while item in todo:
+                j = todo.pop(0)
+                if j == "list":
+                    if t == 0:
+                        wait(PE, e_ed)
+                    for e, ps, c0, _, _ in jobs:
+                        wait(PE, e)
+                        tail.append(to_list(ps, T.ed, T.pd, c0, 64))
+                else:
+                    PE.wait_ge(T.sem["arr%d_%d" % (t, j)], share[j] * (parts[j][1] - parts[j][0]))
+                    e_sum.append(partner_terms(T["psc%d" % (j + 1)], T.land, *parts[j]))
+
+        def pointers():
+            tensor_until("list")
+            if t == 0:
+                wait(V, e_lf)
+            if t + 1 == R:
+                wait(V, e_num)
+            for e, (_, ps, _, like, c0) in zip(tail, jobs):
+                wait(V, e)
+                step(V.tensor_tensor(T.ptf[:, c0:c0 + 64], ps[:, 0:64], like, A.max))
+                ready.append(ev([V.tensor_scalar(T.ptr[:, c0:c0 + 64], T.ptf[:, c0:c0 + 64], 0.25 - RADIX, None, A.add)]))
+
+        news = []
+        for i, (k0, k1) in enumerate([(own, own + 1)] + parts + [(0, 0)]):
+            if i == min(CFG["pg"][t], len(parts) + 1):
                 e_sa = newest()
-            if i == min(CFG["pt"][t], len(spans)):
-                ready += [pointers(*j) for j in jobs]
-            if i == len(spans):
+            if i == min(CFG["pt"][t], len(parts) + 1):
+                pointers()
+            if k1 == 0:
                 break
-            u0, u1 = spans[i]
-            V.wait_ge(T.sem["arr%d_%d" % (t, i)], share * len([d for d in halves[i] if d != me]))
-            if i == 0:
-                wait(V, e_own)
-            e_add = ev([V.tensor_tensor(T.colf[:, c + u0:c + u1], T.own[:, c + u0:c + u1], T.land[:, c + u0:c + u1], A.add)])
-            wait(V, e_add)
-            e_col = ev([V.tensor_copy(T.col[:, c + u0:c + u1], T.colf[:, c + u0:c + u1])])
-            wait(V, e_col)
-            if i == 0:
-                wait(V, e_xm)
-                if t == 0:
-                    wait(V, e_fix, e_gap)
-            ready.append(ev([V.tensor_tensor(T.hist[:, c0 + step * 16 * u0:c0 + step * 16 * u1:step], T.laws[:].indirect(T.col[:, c + u0:c + u1]),
-                                             T.xm[:, b + 16 * u0:b + 16 * u1], A.add)]))
+            if i:
+                tensor_until(i - 1)
+            u0, u1 = 8 * k0, 8 * k1
+            wait(V, e_sum[i])
+            step(V.tensor_copy(T.col[:, c + u0:c + u1], T["psc%d" % i][:, 0:u1 - u0]))
+            if t == 0 and i == 0:
+                wait(V, e_fix, *e_old)
+            if t and i in (0, 2):
+                wait(V, e_old[i // 2])
+            new, looked = T.hist[:, P + b + 16 * u0:P + b + 16 * u1], T.laws[:].indirect(T.col[:, c + u0:c + u1])
+            if t == 0 and late:
+                news.append(V.tensor_copy(new, looked))
+            else:
+                old = T.xs[:, b + 16 * u0:b + 16 * u1] if t else T.x0[:, 16 * u0:16 * u1]
+                news.append(V.tensor_tensor(new, looked, old, A.add))
+        if t == 0:
+            wait(Q, e_sb, e_sum[CFG["p11"]])
+            e_pos[1].append(patch(1, 1))
+        ready.append(ev(news))
 
     f0 = (R - 1) * 64
     wait(V, *ready)
     wait(SC, *ready)
     stores, c0 = [], 0
     for n in CFG["fin"]:
-        cm, c1 = c0 + n // 2, c0 + n
-        e = ev([V.tensor_copy(T.res[:, c0:cm], T.hist[:].indirect(T.ptr[:, f0 + c0 // 16:f0 + cm // 16])),
-                SC.activation(T.res[:, cm:c1], T.hist[:].indirect(T.ptr[:, f0 + cm // 16:f0 + c1 // 16]), F.Copy)])
+        u0, u1 = c0 // 16, (c0 + n) // 16
+        if late:
+            wait(V, e_fld)
+            e = ev([V.tensor_tensor(T.res[:, c0:c0 + n], T.hist[:].indirect(T.ptr[:, f0 + u0:f0 + u1]), T.kind[:, c0:c0 + n], A.add)])
+        else:
+            e = shared(T.res, c0, T.hist[:], lambda a, b: T.ptr[:, f0 + a:f0 + b], u0, u0 + 2 * int((u1 - u0) * CFG["fv"] / 2), u1)
         wait(Q, e)
-        stores.append(Q.dma_start(T.y[:, c0:c1], T.res[:, c0:c1]))
-        c0 = c1
+        stores.append(Q.dma_start(T.y[:, c0:c0 + n], T.res[:, c0:c0 + n]))
+        c0 += n
     wait(Q, ev(stores, 16))
-    g.wait_ge(T.sem.sent, share * (N - 1) * R)
+    g.wait_ge(T.sem.sent, R * sum(s * (k1 - k0) for s, (k0, k1) in zip(share, parts)))
     wait(g, *[e for e in made if e[0] not in waited])

@@ -7,24 +7,39 @@ H = K // 2
 L = S * S
 HIST = P + R * K
 RADIX = 32
+PK = L // 16
 
-CFG = {"late": 0, "gf": [20, 20, 20, 20, 20], "gn": [24, 24, 24, 24, 24], "pgv": [32, 32, 32, 32], "sa": [512, 512, 512, 512, 512],
+CFG = {"late": 0, "old": 0, "gf": [20, 20, 20, 20, 20], "gn": [24, 24, 24, 24, 24], "pgv": [32, 32, 32, 32], "sa": [512, 512, 512, 512, 512],
        "pg": [0, 0, 0, 0, 0], "pm": [1, 1, 1, 1, 1], "pt": [2, 2, 2, 2, 2], "wz": 256, "wv": 0, "wl": 0, "ws": 512, "cv": 512, "x0": 32,
-       "fin": [256, 768, 1024], "fv": 0.5, "near": [3], "dg": 0, "tb": 1, "pk": 1, "p11": -1, "l0": 768}
+       "fin": [256, 768, 1024], "fv": 0.5, "os": [0] * 5, "wg": 0, "b1": 1, "near": [3], "mo": [0] * 5, "mo2": [0] * 5,
+       "dg": 0, "zg": 0, "sl": 0, "pk": 1, "p11": -1, "l0": 768, "th": 0, "nm": 1, "fb": 0, "fs": 0, "tr": [0, 0], "go": [1] * 5, "nk": 0, "c_idh": 4, "fl": 0, "il": 0,
+       "c_sign": 0, "c_wl": 2, "c_tab": 3, "c_taba": 2, "c_dk": 3, "c_id": 4, "c_offs": 4, "c_hi": 4, "c_ed": 4, "c_lf": 4, "c_x0": 4, "tp": 5}
+
+CFG.update({'late': 1, 'sa': [512, 512, 768, 768, 512], 'pg': [0, 0, -1, -1, 0], 'pm': [1, 1, 0, 0, 2], 'pt': [1, 2, 1, 1, 3], 'mo': [1, 0, 0, 0, 0], 'wz': 128, 'wv': 256, 'ws': 0, 'cv': 0, 'fin': [256, 384, 384, 512, 512], 'dg': 1, 'th': 1, 'fb': 2, 'c_id': 0, 'c_offs': 3, 'c_hi': 1, 'c_taba': 3, 'l0': 512})
+
+CFG.update({'pgv': [32, 28, 28, 24], 'sa': [512, 768, 768, 768, 512], 'pg': [0, -1, -1, -1, 0], 'pm': [1, 0, 0, 0, 2], 'pt': [2, 1, 1, 1, 3], 'wz': 128, 'wv': 0, 'ws': 256, 'wg': 512, 'mo': [0] * 5, 'fb': 1, 'c_id': 4, 'c_offs': 3, 'c_hi': 0, 'c_lf': 3, 'tp': 7,
+            'fs': [(0, 384, 'v'), (384, 256, 'v'), (640, 384, 's'), (1664, 384, 's'), (1024, 640, 'v')]})
+
+CFG.update({'late': 1, 'old': 1, 'gf': [16, 16, 20, 16, 20], 'gn': [32, 32, 32, 32, 28], 'pgv': [32, 28, 24, 28], 'sa': [512, 512, 640, 512, 512], 'pg': [0, 0, 0, 0, 1], 'pm': [1, 1, 1, 1, 2], 'pt': [1, 2, 2, 2, 3], 'wz': 128, 'wv': 256, 'wl': 0, 'ws': 0, 'cv': 0, 'os': [1, 1, 1, 1, 0], 'wg': 256, 'b1': 1, 'mo': [1, 0, 0, 0, 0], 'dg': 0, 'l0': 768, 'th': 0, 'fb': 1, 'fs': [(0, 512, 'v'), (512, 512, 's'), (1024, 1024, 'v')], 'c_sign': 0, 'c_tab': 3, 'c_id': 0, 'c_offs': 4, 'c_hi': 4, 'c_ed': 4, 'c_lf': 3, 'tp': 9})
+
+CFG.update({'late': 0, 'old': 1, 'gf': [16] * 5, 'gn': [32] * 5, 'pgv': [20, 28, 28, 28], 'sa': [512] * 5, 'pg': [0] * 5, 'pm': [1, 1, 1, 1, 2], 'pt': [1, 2, 2, 2, 3], 'wz': 128, 'wv': 512, 'wl': 0, 'ws': 0, 'cv': 0, 'fin': [512, 512, 1024], 'fv': 0.45, 'os': [1] * 5, 'wg': 256, 'b1': 1, 'mo': [1, 0, 0, 0, 0], 'dg': 0, 'l0': 0, 'th': 0, 'fb': 1, 'fs': 0, 'nk': 1, 'c_sign': 0, 'c_tab': 3, 'c_id': 3, 'c_offs': 0, 'c_hi': 4, 'c_ed': 4, 'c_lf': 1, 'tp': 7, 'xp': [0] * 5, 'il': 1})
 
 SCRATCH = {
     "la3": ("sbuf", [128, R, 32], "int32"), "lb3": ("sbuf", [128, R, 32], "int32"),
     "lst": ("sbuf", [128, R, 64], "uint16"), "lf": ("sbuf", [128, R, 64], "float32"),
     "hist": ("sbuf", [128, HIST], "bfloat16"), "laws": ("sbuf", [128, 2 * L], "bfloat16"),
-    "where": ("sbuf", [128, P], "float32"), "pos": ("sbuf", [128, (R - 1) * K], "float32"),
+    "pk": ("sbuf", [128, 2 * PK], "bfloat16"), "was": ("sbuf", [128, PK], "bfloat16"), "dk": ("sbuf", [128, 2 * PK], "bfloat16"),
+    "where": ("sbuf", [128, P], "float32"), "pos": ("sbuf", [128, (R - 1) * K + H], "float32"),
     "hi": ("sbuf", [128, 4 * RADIX], "float32"),
     "xs": ("sbuf", [128, R * K], "bfloat16"), "x0": ("sbuf", [128, K], "bfloat16"),
     "pd": ("sbuf", [128, (R - 1) * K + P], "bfloat16"),
     "ptf": ("sbuf", [128, (R - 1) * 64 + 128], "float32"), "ptr": ("sbuf", [128, (R - 1) * 64 + 128], "uint16"),
     "out": ("sbuf", [128, R * 64], "bfloat16"), "land": ("sbuf", [128, R * 64], "bfloat16"),
-    "col": ("sbuf", [128, R * 64], "uint16"), "offs": ("sbuf", [128, 32], "bfloat16"),
-    "pidx": ("sbuf", [128, 1], "int32"), "pm": ("sbuf", [128, 1], "int32"), "cst": ("sbuf", [128, 8], "float32"),
-    "diag": ("sbuf", [128, 144], "float32"), "eb": ("sbuf", [128, 144], "bfloat16"), "ed": ("sbuf", [128, 144], "bfloat16"),
+    "col": ("sbuf", [128, R * 64], "uint16"), "offs": ("sbuf", [128, 40], "bfloat16"),
+    "pidx": ("sbuf", [128, 1], "int32"), "pm": ("sbuf", [128, 1], "int32"), "cst": ("sbuf", [128, 12], "float32"),
+    "ph": ("sbuf", [128, 1], "int32"), "xt": ("sbuf", [128, K], "bfloat16"),
+    "e0": ("sbuf", [128, 160], "bfloat16"), "e1": ("sbuf", [128, 160], "bfloat16"),
+    "diag": ("sbuf", [128, 160], "float32"), "eb": ("sbuf", [128, 144], "bfloat16"), "ed": ("sbuf", [128, 144], "bfloat16"),
     "one": ("sbuf", [128, 128], "bfloat16"), "big": ("sbuf", [128, 128], "bfloat16"),
     "num0": ("sbuf", [128, 128], "float32"), "num": ("sbuf", [128, 128], "float32"),
     "kind": ("sbuf", [128, P], "bfloat16"), "res": ("sbuf", [128, P], "float32"),
@@ -33,7 +48,7 @@ SCRATCH = {
     "psc2": ("psum", [128, 512], "float32"), "psc3": ("psum", [128, 512], "float32"),
     "psp0": ("psum", [128, 512], "float32"), "psp1": ("psum", [128, 512], "float32"),
 }
-SEMAPHORES = ["arr%d_%d" % (t, i) for t in range(R) for i in range(3)] + ["sent", "vv"] + ["e%d" % i for i in range(133)]
+SEMAPHORES = ["arr%d_%d" % (t, i) for t in range(R) for i in range(3)] + ["sent", "vv", "vp"] + ["e%d" % i for i in range(132)]
 
 
 def rank_program(g, core, T, topo):
@@ -41,7 +56,7 @@ def rank_program(g, core, T, topo):
     if me is None:
         return
     V, SC, PE, Q = g.vector, g.scalar, g.tensor, g.sync
-    made, waited, steps = [], {}, [0]
+    made, waited, steps = [], {}, [0, 0]
 
     def ev(calls, n=1):
         name = "e%d" % len(made)
@@ -86,77 +101,164 @@ def rank_program(g, core, T, topo):
     order = blocks(me)
     own = order.index(me)
     eng = topo.engines(core, T.cores[order[-1]])
-    parts, k0 = [(own + 1, N)], 0
+    parts, k0 = [(own + 1, N, 0)], 0
     for n in CFG["near"]:
-        parts.append((k0, k0 + n))
+        parts.append((k0, k0 + n, 1))
         k0 += n
-    share = [len(eng) // (1 << (k1 - k0 - 1).bit_length()) for k0, k1 in parts]
+    share = [len(eng) // (1 << (k1 - k0 - 1).bit_length()) for k0, k1, _ in parts]
 
-    late, wz, l0 = CFG["late"], CFG["wz"], CFG["l0"]
+    late, wz, l0, xm, dl, th = CFG["late"], CFG["wz"], CFG["l0"], CFG["old"] == 1, CFG["old"] == 2, CFG["th"]
     wv = wz + CFG["wv"]
     wl = wv + CFG["wl"]
     ws = wl + CFG["ws"]
     e_la = ev([Q.dma_start(T.la3[:], T.la[:]), SC.dma_start(T.lb3[:], T.lb[:])], 16)
-    early = [Q.dma_start(T.laws[:, 0:l0], T.law[:, 0:l0])] if l0 else []
-    e_w0 = ev([V.memset(T.where[:, 0:wz], 0.0)])
-    first = T.hist if late else T.kind
-    e_sp0 = ev([V.memset(first[:, 0:P], 0.0)])
-    wait(Q, e_sp0)
-    e_sp = ev([Q.dma_start(first[0:128:16, 0:P], T.fld[0:128:16, :])], 16)
-    e_fl = []
+    tr, nk = CFG["tr"], CFG["nk"]
+    if nk:
+        e_sp = ev([Q.dma_start(T.hist[:, 0:P], T.fld[:])], 16)
+    e_lawa = [ev([Q.dma_start(T.laws[:, 0:l0], T.law[:, 0:l0])], 16)] if l0 else []
+    e_w0 = iota(T.where[:, 0:wz], [[0, wz]], 0, 0) if CFG["zg"] else ev([V.memset(T.where[:, 0:wz], 0.0)])
+    first = T.hist if late or nk else T.kind
+    if not nk:
+        e_sp0 = ev([V.memset(first[:, 0:P], 0.0)])
+        wait(Q, e_sp0)
+        e_sp = ev([Q.dma_start(first[0:128:16, 0:P], T.fld[0:128:16, :])], 16)
 
     def law():
-        return ev(early + [Q.dma_start(T.laws[:, l0:L], T.law[:, l0:L])], 16)
+        pk = ev([Q.dma_start(T.pk[:, i * PK:(i + 1) * PK], T.law[i:128:16, :]) for i in range(2)], 16) if dl else None
+        return pk, ev([Q.dma_start(T.laws[:, l0:L], T.law[:, l0:L])], 16)
 
     if CFG["pk"] == 0:
-        e_law = law()
+        e_pk, e_law = law()
 
     low = [[0, H // RADIX], [1, RADIX]]
     e_p = ev([g.iota(T.pidx[:], [[0, 1]], 0, 1)])
     if CFG["dg"]:
-        e_diag = iota(T.diag[:], [[1, 144]], -16, -1)
-    e_lo = [iota(T.pos[:, 0:H], low, RADIX, 0)]
+        e_diag = iota(T.diag[:], [[1, 160]], -16, -1)
+    e_lo = [iota(T.pos[:, H:K], low, RADIX, 0)]
     if not CFG["dg"]:
-        e_diag = iota(T.diag[:], [[1, 144]], -16, -1)
-    e_lo.append(iota(T.pos[:, H:K], low, RADIX, 0))
+        e_diag = iota(T.diag[:], [[1, 160]], -16, -1)
+    wg = P - CFG["wg"]
+    e_wg = [iota(T.where[:, wg:P], [[0, P - wg]], 0, 0)] if wg < P else []
+    e_lo.append(iota(T.pos[:, K:K + H], low, RADIX, 0))
+    if dl:
+        e_was = iota(T.was[:], [[0, PK // S], [1, S]], 0, 0)
+
+    def upper(c0, n, first):
+        return iota(T.pos[:, c0:c0 + n], [[1, n // RADIX], [0, RADIX]], first // RADIX, 0)
+
+    if CFG["b1"]:
+        e_b1 = upper(0, H, P + K)
     wait(SC, e_w0)
 
     def zero(c0, c1):
         return ev([SC.activation(T.where[:, c:min(c1, c + wz)], T.where[:, 0:min(wz, c1 - c)], F.Silu) for c in range(c0, c1, wz)])
 
-    e_w2 = zero(ws, P)
+    e_w2 = zero(ws, wg)
     wait(V, e_p)
     step(V.tensor_scalar(T.pm[:], T.pidx[:], 15, None, A.bitwise_and))
-    row0, sign, pmf, keep, neg, wt, wd = (T.cst[:, i:i + 1] for i in range(7))
-    step(V.tensor_copy(pmf, T.pm[:]), V.tensor_scalar(row0, T.pm[:], 0.0, None, A.is_equal))
+    row0, sign, pmf, keep, neg, wt, wd, w0, w1 = (T.cst[:, i:i + 1] for i in range(9))
+    step(V.tensor_copy(pmf, T.pm[:]), *[V.tensor_scalar(row0, T.pm[:], 0.0, None, A.is_equal) for _ in range(0 in tr)])
     wait(V, e_w0)
 
     def high(t):
         src, add = (T.hi[:, 0:RADIX], 0.0) if t else (T.where[:, 0:RADIX], pmf)
         return ev([V.tensor_scalar(T.hi[:, RADIX * j:RADIX * (j + 1)], src, add, float(16 * j + (0 if t else P // RADIX)), A.add, A.add)
-                   for j in (2 * t, 2 * t + 1)])
+                   for j in ((3,) if t else (0, 1))])
 
-    def patch(t, h):
-        j = 2 * t + h
-        return ev([Q.dma_start(T.pos[0:128:16, h * H:h * H + H], T.hi[:, RADIX * j:RADIX * (j + 1)])], 16)
+    def patch(j, c0):
+        return ev([Q.dma_start(T.pos[0:128:16, c0:c0 + H], T.hi[:, RADIX * j:RADIX * (j + 1)])], 16)
+
+    def lower(c0, n):
+        return ev([Q.dma_start(T.pos[1:128:16, c0:c0 + n], T.pos[1:128:16, H:H + n])], 16)
 
     def eye():
         wait(V, e_diag)
-        return ev([V.tensor_scalar(T.eb[:], T.diag[:], 0.0, row0, A.is_equal, A.mult)])
+        return ev([V.tensor_scalar(T.eb[:], T.diag[:, 0:144], 0.0, row0, A.is_equal, A.mult)]) if 0 in tr else None
+
+    def tables(c0, c1):
+        e = ev([V.tensor_scalar(T.laws[:, L + c0:L + c1], T.laws[:, c0:c1], sign, None, A.mult)])
+        wait(Q, e)
+        if dl:
+            wait(Q, done["dk"])
+            calls = [Q.dma_start(T.laws[0:128:16, i * L:(i + 1) * L], T.dk[:, i * PK:(i + 1) * PK]) for i in range(2)]
+        else:
+            calls = [Q.dma_start(T.laws[0:128:16, L + c0:L + c1], T.law[1:128:16, c0:c1])]
+        return ev(calls + [Q.dma_start(T.laws[1:128:16, c0:c1], T.laws[1:128:16, L + c0:L + c1])], 16)
 
     e_hi = {0: high(0)}
-    e_cst = ev([V.tensor_scalar(sign, T.pm[:], 2.0, -1.0, A.is_ge, A.mult)])
     e_w1 = [ev([V.memset(T.where[:, wz:wv], 0.0)])] if wv > wz else []
     if CFG["dg"]:
         e_eb = eye()
+    done = {}
+
+    def chore(name):
+        if name == "id":
+            wait(V, e_diag)
+            return ev([V.tensor_scalar(T.one[:], T.diag[:, 16:144], 0.0, None, A.is_equal)] +
+                      [V.tensor_scalar(T.big[:], T.diag[:, 16:144], 0.0, float(S), A.is_equal, A.mult) for _ in range(0 in tr)])
+        if name == "idh":
+            wait(V, e_diag)
+            step(V.tensor_scalar(T.ph[:], T.pidx[:], 16, None, A.bitwise_and))
+            step(V.tensor_scalar(w0, T.ph[:], 0.0, float(S), A.is_equal, A.mult), V.tensor_scalar(w1, T.ph[:], 0.0, None, A.not_equal))
+            return ev([V.tensor_scalar(T.e0[:], T.diag[:], 0.0, w0, A.is_equal, A.mult),
+                       V.tensor_scalar(T.e1[:], T.diag[:], 0.0, w1, A.is_equal, A.mult)])
+        if name == "offs":
+            return ev([V.memset(T.offs[:, 0:40:2], 0.0), V.memset(T.offs[:, 1:40:2], float(L))])
+        if name == "hi":
+            wait(V, e_hi[0])
+            return high(1)
+        if name == "ed":
+            wait(V, e_diag)
+            step(V.tensor_scalar(neg, T.pm[:], -1.0, None, A.mult),
+                 V.tensor_scalar(wt, T.pm[:], 1.0 - RADIX, float(RADIX), A.mult, A.add))
+            step(V.tensor_scalar(wd, wt, 0.0, None, A.max))
+            return ev([V.tensor_scalar(T.ed[:], T.diag[:, 0:144], neg, wd, A.is_equal, A.mult)])
+        if name == "lf":
+            wait(V, *e_lst)
+            return ev([V.tensor_scalar(T.lf[:, 1:R, :], T.lst[:, 1:R, :], float(RADIX), None, A.add)])
+        if name == "wl":
+            return ev([V.memset(T.where[:, wv:wl], 0.0)])
+        if name == "sign":
+            more = [V.tensor_scalar(keep, T.pm[:], -float(PK // S), None, A.mult)] if dl else \
+                [V.tensor_scalar(keep, T.pm[:], 0.0, None, A.not_equal)] if xm or not late else []
+            return ev([V.tensor_scalar(sign, T.pm[:], 2.0, -1.0, A.is_ge, A.mult)] + more)
+        if name == "dk":
+            wait(V, e_pk, e_was, done["sign"])
+            return ev([V.tensor_tensor(T.dk[:, PK:2 * PK], T.pk[:, PK:2 * PK], T.was[:], A.subtract)] +
+                      [V.tensor_scalar(T.dk[:, i * S:(i + 1) * S], T.pk[:, i * S:(i + 1) * S], keep, -float(i), A.add, A.add)
+                       for i in range(PK // S)])
+        if name == "taba":
+            wait(V, *e_lawa, done["sign"])
+            return tables(0, l0)
+        if name == "tab":
+            wait(V, e_law, *e_lawa, done["sign"])
+            return tables(l0 if th else 0, L)
+        wait(V, e_fld, done["sign"])
+        win = T.hist[:, 0:P].indirect(T.lst[:, 0, 0:CFG["x0"]])
+        o = T.x0[:, 0:16 * CFG["x0"]]
+        return ev([V.tensor_copy(o, win) if dl else V.tensor_scalar(o, win, keep, None, A.mult)])
+
+    def chores(slot):
+        names = ["wl", "hi", "sign", "dk", "taba", "offs", "id", "idh", "ed", "lf", "x0"]
+        names.insert(CFG["tp"], "tab")
+        skip = ["wl"] * (wl == wv) + ["x0"] * (late or nk) + ["dk"] * (not dl) + ["taba"] * (not th) + ["idh"] * (1 not in tr)
+        for name in names:
+            if CFG["c_" + name] == slot and name not in skip:
+                done[name] = chore(name)
+
+    chores(0)
     wait(Q, e_hi[0], e_lo[0])
-    e_pos = {0: [patch(0, 0)]}
+    e_pos = {0: [patch(0, H)]}
     if CFG["pk"] == 1:
-        e_law = law()
+        e_pk, e_law = law()
     wait(Q, e_lo[1])
-    e_pos[0].append(patch(0, 1))
-    if not late:
-        e_fld = ev([Q.dma_start(T.hist[:, 0:P], T.fld[:])], 16)
+    e_pos[0].append(patch(1, K))
+    pieces = []
+    if not nk and not (late and CFG["fl"]):
+        e_fld = ev([Q.dma_start(T.kind[:] if late else T.hist[:, 0:P], T.fld[:])], 16)
+    if CFG["b1"]:
+        wait(Q, e_b1)
+        e_pos[1] = [lower(0, H)]
 
     def moves(k0, k1):
         calls = []
@@ -171,66 +273,137 @@ def rank_program(g, core, T, topo):
         return ev(calls)
 
     wait(V, e_la)
-    e_lst = moves(0, N)
+    e_lst = [moves(own + CFG["os"][0], N) if CFG["sl"] else moves(0, N)]
     if not CFG["dg"]:
         e_eb = eye()
+    chores(1)
 
     def scatter(t, a, b):
-        c0 = max(t - 1, 0) * K
+        c0 = (t - 1) * K + H if t > 1 else H - t * H
         return ev([SC.activation(T.where[:].indirect(T.lst[:, t, a // 16:b // 16]), T.pos[:, c0 + a:c0 + b], F.Silu)])
 
-    def tables():
-        wait(V, e_law, e_cst)
-        e = ev([V.tensor_scalar(T.laws[:, L:2 * L], T.laws[:, 0:L], sign, None, A.mult)])
-        wait(Q, e)
-        return ev([Q.dma_start(T.laws[0:128:16, L:2 * L], T.law[1:128:16, :]),
-                   Q.dma_start(T.laws[1:128:16, 0:L], T.laws[1:128:16, L:2 * L])], 16)
-
-    spans = [(8 * own, 64), (0, 8 * own)]
-    ready, e_sa, e_sb = [e_sp, e_lst], None, None
+    ready, e_sa, e_sb = [e_sp, e_lst[0]], None, None
     for t in range(R):
         b, c = t * K, t * 64
+        mine = CFG["os"][t]
+        spans = [(8 * (own + mine), 64), (0, 8 * (own + mine))]
         if t:
             win, off = T.hist[:, 0:P + t * K], lambda u0, u1: T.ptr[:, c - 64 + u0:c - 64 + u1]
         else:
             win, off = first[:, 0:P], lambda u0, u1: T.lst[:, 0, u0:u1]
         if 0 < t < R - 1:
             wait(Q, ready[-1], e_hi[t + 1])
-            e_pos[t + 1] = [ev([Q.dma_start(T.pos[1:128:16, t * K:(t + 1) * K], T.pos[1:128:16, 0:K])], 16)] * 2
-            if late and t < 3:
-                e_fl.append(Q.dma_start(T.kind[:, (t - 1) * K:t * K], T.fld[:, (t - 1) * K:t * K]))
-            if late and t == 3:
-                wait(Q, ev(e_fl, 16))
-                e_fld = ev([Q.dma_start(T.kind[0:128:16, :], T.hist[1:128:16, 0:P])], 16)
+            e_pos[t + 1] = [lower(t * K + H, K)] * 2
+            if late and CFG["fl"]:
+                c0, c1 = (t - 1) * 704, min(P, t * 704)
+                pieces.append(Q.dma_start(T.kind[:, c0:c1], T.fld[:, c0:c1]))
+        if late and t == (R - 1 if CFG["fl"] else 1):
+            wait(Q, ev(pieces, 16) if pieces else e_fld)
+            e_fld = ev([Q.dma_start(T.kind[0:128:16, :], T.hist[1:128:16, 0:P])], 16)
         wait(V, *ready)
         wait(SC, *ready)
-        e_x, e_mm, e_out, e_old = [], [], [], []
-        for i, (u0, u1) in enumerate(spans):
-            e_x.append(shared(T.xs, b + 16 * u0, win, off, u0, u0 + CFG["gn" if i else "gf"][t], u1))
-        if t == 0:
+        e_x, e_mm, e_out, e_old, jobs, ready, tail = [], [], [], [], [], [], []
+        e_x, e_mm, part_x, go = {}, {}, {}, CFG["go"][t]
+        e_old = [None, None] if t else []
+
+        def forget(c0, c1):
+            src = T.laws[1:128:16, L + c0:L + c1] if nk else first[1:128:16, c0:c1]
+            return ev([Q.dma_start(T.xs[0:128:16, b + c0:b + c1], src)], 16)
+
+        def masked(u0, u1):
+            wait(V, *e_x.values(), done["sign"])
+            return ev([V.tensor_scalar(T.x0[:, 16 * u0:16 * u1], T.xs[:, b + 16 * u0:b + 16 * u1], keep, None, A.mult)])
+
+        def gather(i, who):
+            u0, u1 = spans[i]
+            um = min(u1, u0 + CFG["gn" if i else "gf"][t])
+            if who and um < u1:
+                part_x[i] = [SC.activation(T.xs[:, b + 16 * um:b + 16 * u1], win.indirect(off(um, u1)), F.Copy)]
+            if not who:
+                e_x[i] = ev(part_x.get(i, []) + [V.tensor_copy(T.xs[:, b + 16 * u0:b + 16 * um], win.indirect(off(u0, um)))])
+
+        def listed(i):
+            u0, u1 = spans[i]
+            if tr[i]:
+                wait(V, e_x[i])
+                e_mm[i] = ev([V.transpose(T.xt[:, 16 * u0:16 * u1], T.xs[:, b + 16 * u0:b + 16 * u1])])
+            else:
+                wait(PE, e_x[i])
+                e_mm[i] = to_list(T["psa%d" % i], T.eb, T.xs, b + 16 * u0, u1 - u0)
+            if t and CFG["old"] == 0:
+                wait(Q, e_mm[i])
+                e_old[i] = forget(16 * u0, 16 * u1)
+
+        if t == 0 and 0 in tr:
             wait(PE, e_eb)
+        for i in ((1, 0) if go == 2 else (0, 1)):
+            if t == 0 and i == 1 and CFG["sl"]:
+                e_lst.append(moves(0, spans[1][1] // 8))
+                wait(V, e_lst[1])
+                wait(SC, e_lst[1])
+            gather(i, 1)
+            if go or i == 0:
+                gather(i, 0)
+                if not tr[i]:
+                    listed(i)
+        if t == 0:
             if ws > wl:
                 e_w1.append(zero(wl, ws))
-            if wl > wv:
-                e_w1.append(ev([V.memset(T.where[:, wv:wl], 0.0)]))
+            chores(2)
+        if dl and t:
+            e_old = e_x
+
+        sa = CFG["sa"][t]
+        if t == 0:
+            wait(SC, e_pos[0][0], e_w2, e_hi[0], *e_w1, *e_wg, *([done["wl"]] if wl > wv else []))
+            e_sa = scatter(0, 0, sa)
+        wait(SC, e_sa, *e_pos[t])
+        e_sb = scatter(t, sa, K) if sa < K else e_sa
+
+        def newest():
+            if CFG["pgv"][t] if t + 1 < R else CFG["cv"]:
+                wait(V, e_sb)
+            wait(SC, e_sb)
+            if t + 1 < R:
+                e_pg = shared(T.pd, b, T.where[:], lambda u0, u1: T.lst[:, t + 1, u0:u1], 0, CFG["pgv"][t], 64)
+                jobs.append((e_pg, T["psp%d" % (t % 2)], b, T.lf[:, t + 1, :], c))
+                n0 = CFG["x0"]
+                if t == 0 and not late and not nk and n0 < 64:
+                    wait(SC, e_fld, done["sign"])
+                    rest = T.x0[:, 16 * n0:K], T.hist[:, 0:P].indirect(off(n0, 64)), F.Copy
+                    e_old.append(ev([SC.activation(*rest) if dl else SC.activation(*rest, scale=keep)]))
+                n = CFG["sa"][t + 1]
+                if n == 0:
+                    return e_pg
+                wait(SC, e_pg, *e_pos[t + 1][:1 + (n > H)])
+                return scatter(t + 1, 0, n)
+            cv = CFG["cv"]
+            for u in range(2):
+                a = u * K
+                calls = [V.tensor_copy(T.pd[:, b + a:b + a + cv], T.where[:, a:a + cv])] if cv else []
+                if cv < K:
+                    calls.append(SC.activation(T.pd[:, b + a + cv:b + a + K], T.where[:, a + cv:a + K], F.Copy))
+                jobs.append((ev(calls), T["psp%d" % u], b + a, T.num[:, 64 * u:64 * u + 64], c + 64 * u))
+            return None
+
         for i, (u0, u1) in enumerate(spans):
-            wait(PE, e_x[i])
-            e_mm.append(to_list(T["psa%d" % i], T.eb, T.xs, b + 16 * u0, u1 - u0))
-            if t:
-                wait(Q, e_mm[i])
-                e_old.append(ev([Q.dma_start(T.xs[0:128:16, b + 16 * u0:b + 16 * u1], first[1:128:16, 16 * u0:16 * u1])], 16))
-        for i, (u0, u1) in enumerate(spans):
-            if t == 0 and i == 1 and CFG["tb"]:
-                e_fix = tables()
-            if t == R - 1 and i == 1:
-                wait(V, e_num0)
-                e_num = ev([V.tensor_scalar(T.num[:], T.num0[:], pmf, None, A.add)])
+            if t == 0 and i == 1:
+                chores(3)
+            if i not in e_x:
+                gather(i, 0)
+            if i not in e_mm:
+                listed(i)
+            if xm and (t or nk) and i == 1 and CFG["xp"][t] < 2:
+                e_old = [masked(0, 64)] * 2 if CFG["xp"][t] == 0 else [masked(*spans[0])]
+            if i == 1 and CFG["pg"][t] < 0:
+                e_sa = newest()
             wait(V, e_mm[i])
-            e_out.append(ev([V.tensor_copy(T.out[:, c + u0:c + u1], T["psa%d" % i][:, 0:u1 - u0])]))
+            src = T.xt[:, 16 * u0:16 * u1:16] if tr[i] else T["psa%d" % i][:, 0:u1 - u0]
+            e_out.append(ev([V.tensor_copy(T.out[:, c + u0:c + u1], src)]))
             wait(g, e_out[i])
-            for j in ([0] if i == 0 else range(1, len(parts))):
+            for j in [j for j, part in enumerate(parts) if part[2] == i]:
                 transfers = []
-                for n, k in enumerate(range(*parts[j])):
+                for n, k in enumerate(range(*parts[j][:2])):
                     d = order[k]
                     rid, pid, _ = topo.addr(T.cores[d])
                     at = c + 8 * blocks(d).index(me)
@@ -239,83 +412,68 @@ def rank_program(g, core, T, topo):
                                                        remote_sem=T.sem["arr%d_%d" % (t, j)], src=T.out[:, c + 8 * k:c + 8 * k + 8],
                                                        dst=T.land[:, at:at + 8]))
                 g.remote_dma_fused(transfers, local_sem=T.sem.sent)
+        if xm and (t or nk) and CFG["xp"][t]:
+            e_old = [masked(0, 64)] * 2 if CFG["xp"][t] == 2 else e_old + [masked(*spans[1])]
+        if t == 0 and not CFG["b1"]:
+            e_b1 = upper(0, H, P + K)
         if t + 2 < R:
-            e_hi[t + 2] = iota(T.pos[:, (t + 1) * K:(t + 2) * K], [[1, K // RADIX], [0, RADIX]], (P + (t + 2) * K) // RADIX, 0)
+            e_hi[t + 2] = upper((t + 1) * K + H, K, P + (t + 2) * K)
         elif t + 2 == R:
             e_num0 = iota(T.num0[:], [[16, 128]], RADIX, 0)
+        if t == R - 2 + CFG["nm"]:
+            wait(V, e_num0)
+            e_num = ev([V.tensor_scalar(T.num[:], T.num0[:], pmf, None, A.add)])
 
-        sa = CFG["sa"][t]
-        if t == 0:
-            wait(SC, e_pos[0][0], e_w2, e_hi[0], *e_w1)
-            e_sa = scatter(0, 0, sa)
-        wait(SC, e_sa, *e_pos[t])
-        e_sb = scatter(t, sa, K) if sa < K else e_sa
-
-        def own_terms(ps, k0, k1):
+        def own_terms(ps, k0, k1, mixed):
             n, a = 8 * (k1 - k0), c + 8 * k0
             PE.matmul(ps[:, 0:n], T.one[:], T.offs[:, 0:n], True, False)
+            if mixed:
+                for y in range(2):
+                    PE.matmul(ps[:, 0:n:2], T.e0[:, 16 - 16 * y:144 - 16 * y], T.out[:, a + y:a + n:2], False, False)
+                    PE.matmul(ps[:, 1:n:2], T.e1[:, 32 - 16 * y:160 - 16 * y], T.out[:, a + y:a + n:2], False, False)
+                return
             PE.matmul(ps[:, 0:n:2], T.big[:], T.out[:, a:a + n:2], False, False)
             PE.matmul(ps[:, 1:n:2], T.one[:], T.out[:, a + 1:a + n:2], False, False)
 
-        def partner_terms(ps, src, k0, k1):
+        def partner_terms(ps, o, src, k0, k1, last, mixed):
             n, a = 8 * (k1 - k0), c + 8 * k0
-            PE.matmul(ps[:, 0:n:2], T.one[:], src[:, a + 1:a + n:2], False, False)
-            return ev([PE.matmul(ps[:, 1:n:2], T.big[:], src[:, a:a + n:2], False, True)])
+            if mixed:
+                for y in range(2):
+                    PE.matmul(ps[:, o:o + n:2], T.e1[:, 32 - 16 * y:160 - 16 * y], src[:, a + y:a + n:2], False, False)
+                    call = PE.matmul(ps[:, o + 1:o + n:2], T.e0[:, 16 - 16 * y:144 - 16 * y], src[:, a + y:a + n:2], False, last and y == 1)
+                return ev([call]) if last else None
+            PE.matmul(ps[:, o:o + n:2], T.one[:], src[:, a + 1:a + n:2], False, False)
+            call = PE.matmul(ps[:, o + 1:o + n:2], T.big[:], src[:, a:a + n:2], False, last)
+            return ev([call]) if last else None
+
+        looks = [(k0, k1, j, span) for j, (k0, k1, span) in enumerate(parts)]
+        if CFG["mo"][t]:
+            looks = [(min(k0, own), max(k1, own + 1), j, span) if span == mine and (k1 == own or k0 == own + 1) else (k0, k1, j, span)
+                     for k0, k1, j, span in looks]
+        else:
+            looks.insert(CFG["mo2"][t], (own, own + 1, None, mine))
 
         if t == 0:
-            if not CFG["tb"]:
-                e_fix = tables()
-            e_id = ev([V.tensor_scalar(T.one[:], T.diag[:, 16:144], 0.0, None, A.is_equal),
-                       V.tensor_scalar(T.big[:], T.diag[:, 16:144], 0.0, float(S), A.is_equal, A.mult),
-                       V.memset(T.offs[:, 0:32:2], 0.0), V.memset(T.offs[:, 1:32:2], float(L))])
-            wait(V, e_hi[0])
-            e_hi[1] = high(1)
-            wait(Q, e_hi[1], e_sa)
-            e_pos[1] = [patch(1, 0)]
-            wait(PE, e_id)
-        wait(PE, *e_out)
-        own_terms(T.psc0, own, own + 1)
-        e_sum = [partner_terms(T.psc0, T.out, own, own + 1)]
-        for j, part in enumerate(parts):
-            own_terms(T["psc%d" % (j + 1)], *part)
+            chores(4)
+            wait(Q, done["hi"], e_sa)
+            e_second = patch(3, H)
+            if not CFG["b1"]:
+                wait(Q, e_b1)
+                e_pos[1] = [lower(0, H)]
+            e_pos[1].append(e_second)
+            wait(PE, *[done[n] for n in ("id", "offs", "idh") if n in done])
+            if nk and CFG["old"] == 0:
+                wait(Q, *e_mm.values())
+                done["x0"] = forget(0, K)
+            e_old = e_old + [done[n] for n in ("tab", "taba", "x0") if n in done]
+        e_sum = {}
+        for i, (k0, k1, j, span) in sorted(enumerate(looks), key=lambda x: (x[1][3], x[1][2] is not None)):
+            wait(PE, e_out[span])
+            own_terms(T["psc%d" % i], k0, k1, tr[span])
+            if k0 <= own < k1:
+                e_sum[i] = partner_terms(T["psc%d" % i], 8 * (own - k0), T.out, own, own + 1, j is None, tr[span])
 
-        if t == 0:
-            step(V.tensor_scalar(neg, T.pm[:], -1.0, None, A.mult),
-                 V.tensor_scalar(keep, T.pm[:], 0.0, None, A.not_equal),
-                 V.tensor_scalar(wt, T.pm[:], 1.0 - RADIX, float(RADIX), A.mult, A.add))
-            step(V.tensor_scalar(wd, wt, 0.0, None, A.max))
-            e_ed = ev([V.tensor_scalar(T.ed[:], T.diag[:], neg, wd, A.is_equal, A.mult)])
-            e_lf = ev([V.tensor_scalar(T.lf[:, 1:R, :], T.lst[:, 1:R, :], float(RADIX), None, A.add)])
-            if not late:
-                wait(V, e_fld)
-                n0 = CFG["x0"]
-                e_old = [ev([V.tensor_scalar(T.x0[:, 0:16 * n0], T.hist[:, 0:P].indirect(off(0, n0)), keep, None, A.mult)])]
-        jobs, ready, tail = [], [], []
-
-        def newest():
-            wait(V, e_sb)
-            wait(SC, e_sb)
-            if t + 1 < R:
-                e_pg = shared(T.pd, b, T.where[:], lambda u0, u1: T.lst[:, t + 1, u0:u1], 0, CFG["pgv"][t], 64)
-                jobs.append((e_pg, T["psp%d" % (t % 2)], b, T.lf[:, t + 1, :], c))
-                if t == 0 and not late and CFG["x0"] < 64:
-                    wait(SC, e_fld, e_ed)
-                    e_old.append(ev([SC.activation(T.x0[:, 16 * n0:K], T.hist[:, 0:P].indirect(off(n0, 64)), F.Copy, scale=keep)]))
-                n = CFG["sa"][t + 1]
-                if n == 0:
-                    return e_pg
-                wait(SC, e_pg, e_pos[t + 1][0])
-                return scatter(t + 1, 0, n)
-            cv = CFG["cv"]
-            for u in range(2):
-                a = u * K
-                calls = [V.tensor_copy(T.pd[:, b + a:b + a + cv], T.where[:, a:a + cv])]
-                if cv < K:
-                    calls.append(SC.activation(T.pd[:, b + a + cv:b + a + K], T.where[:, a + cv:a + K], F.Copy))
-                jobs.append((ev(calls), T["psp%d" % u], b + a, T.num[:, 64 * u:64 * u + 64], c + 64 * u))
-            return None
-
-        todo = list(range(len(parts)))
+        todo = [i for i, x in enumerate(looks) if x[2] is not None]
         todo.insert(min(CFG["pm"][t], len(parts)), "list")
 
         def tensor_until(item):
@@ -323,59 +481,112 @@ def rank_program(g, core, T, topo):
                 j = todo.pop(0)
                 if j == "list":
                     if t == 0:
-                        wait(PE, e_ed)
+                        wait(PE, done["ed"])
                     for e, ps, c0, _, _ in jobs:
                         wait(PE, e)
                         tail.append(to_list(ps, T.ed, T.pd, c0, 64))
                 else:
-                    PE.wait_ge(T.sem["arr%d_%d" % (t, j)], share[j] * (parts[j][1] - parts[j][0]))
-                    e_sum.append(partner_terms(T["psc%d" % (j + 1)], T.land, *parts[j]))
+                    k0, _, r, _ = looks[j]
+                    PE.wait_ge(T.sem["arr%d_%d" % (t, r)], share[r] * (parts[r][1] - parts[r][0]))
+                    e_sum[j] = partner_terms(T["psc%d" % j], 8 * (parts[r][0] - k0), T.land, parts[r][0], parts[r][1], True, tr[parts[r][2]])
 
-        def pointers():
-            tensor_until("list")
-            if t == 0:
-                wait(V, e_lf)
-            if t + 1 == R:
-                wait(V, e_num)
-            for e, (_, ps, _, like, c0) in zip(tail, jobs):
-                wait(V, e)
-                step(V.tensor_tensor(T.ptf[:, c0:c0 + 64], ps[:, 0:64], like, A.max))
-                ready.append(ev([V.tensor_scalar(T.ptr[:, c0:c0 + 64], T.ptf[:, c0:c0 + 64], 0.25 - RADIX, None, A.add)]))
+        def larger(u):
+            _, ps, _, like, c0 = jobs[u]
+            wait(V, tail[u])
+            V.tensor_tensor(T.ptf[:, c0:c0 + 64], ps[:, 0:64], like, A.max).then_inc(T.sem.vp, 1)
+            steps[1] += 1
+
+        def whole(u):
+            c0 = jobs[u][4]
+            V.wait_ge(T.sem.vp, steps[1])
+            return ev([V.tensor_scalar(T.ptr[:, c0:c0 + 64], T.ptf[:, c0:c0 + 64], 0.25 - RADIX, None, A.add)])
+
+        def pointer(u):
+            larger(u)
+            return whole(u)
 
         news = []
-        for i, (k0, k1) in enumerate([(own, own + 1)] + parts + [(0, 0)]):
-            if i == min(CFG["pg"][t], len(parts) + 1):
+        for i, (k0, k1, j, span) in enumerate(looks + [(0, 0, 0, 0)]):
+            if i == min(CFG["pg"][t], len(looks)):
                 e_sa = newest()
-            if i == min(CFG["pt"][t], len(parts) + 1):
-                pointers()
+            now = i == min(CFG["pt"][t], len(looks))
+            if now:
+                tensor_until("list")
+                if t == 0:
+                    wait(V, done["lf"])
+                if t + 1 == R:
+                    wait(V, e_num)
+                if t + 1 == R and not CFG["fb"]:
+                    ready.append(pointer(1))
+                larger(0)
+            if k1 == 0 or not CFG["il"]:
+                if now:
+                    ready.append(whole(0))
+                now = False
             if k1 == 0:
                 break
-            if i:
-                tensor_until(i - 1)
+            tensor_until(i)
             u0, u1 = 8 * k0, 8 * k1
             wait(V, e_sum[i])
-            step(V.tensor_copy(T.col[:, c + u0:c + u1], T["psc%d" % i][:, 0:u1 - u0]))
+            V.tensor_copy(T.col[:, c + u0:c + u1], T["psc%d" % i][:, 0:u1 - u0]).then_inc(T.sem.vv, 1)
+            steps[0] += 1
+            if now:
+                ready.append(whole(0))
+            V.wait_ge(T.sem.vv, steps[0])
             if t == 0 and i == 0:
-                wait(V, e_fix, *e_old)
-            if t and i in (0, 2):
-                wait(V, e_old[i // 2])
+                wait(V, *e_old)
+            if t:
+                wait(V, e_old[span])
             new, looked = T.hist[:, P + b + 16 * u0:P + b + 16 * u1], T.laws[:].indirect(T.col[:, c + u0:c + u1])
-            if t == 0 and late:
+            if t == 0 and late and not dl:
                 news.append(V.tensor_copy(new, looked))
             else:
-                old = T.xs[:, b + 16 * u0:b + 16 * u1] if t else T.x0[:, 16 * u0:16 * u1]
+                old = T.xs[:, b + 16 * u0:b + 16 * u1] if (t or late or nk) and not xm else T.x0[:, 16 * u0:16 * u1]
                 news.append(V.tensor_tensor(new, looked, old, A.add))
-        if t == 0:
-            wait(Q, e_sb, e_sum[CFG["p11"]])
-            e_pos[1].append(patch(1, 1))
         ready.append(ev(news))
 
     f0 = (R - 1) * 64
     wait(V, *ready)
     wait(SC, *ready)
     stores, c0 = [], 0
-    for n in CFG["fin"]:
+    if CFG["fs"]:
+        wait(V, e_fld)
+        wait(PE, e_fld)
+        e_half, evs, late_s = None, {}, []
+        for i, (c0, n, who) in enumerate(CFG["fs"]):
+            if who == "v":
+                if c0 >= K and e_half is None:
+                    e_half = pointer(1)
+                    wait(V, e_half)
+                evs[i] = ev([V.tensor_tensor(T.res[:, c0:c0 + n], T.hist[:].indirect(T.ptr[:, f0 + c0 // 16:f0 + (c0 + n) // 16]),
+                                             T.kind[:, c0:c0 + n], A.add)])
+                if i == CFG["fb"] - 1 and e_half is None:
+                    e_half = pointer(1)
+                    wait(V, e_half)
+        for i, (c0, n, who) in enumerate(CFG["fs"]):
+            if who == "s":
+                if c0 >= K:
+                    wait(SC, e_half)
+                ps = T["psa%d" % (len(late_s) % 2)]
+                e = ev([SC.activation(T.xs[:, c0:c0 + n], T.hist[:].indirect(T.ptr[:, f0 + c0 // 16:f0 + (c0 + n) // 16]), F.Copy)])
+                PE.matmul(ps[:, 0:n], T.one[:], T.kind[:, c0:c0 + n], True, False)
+                wait(PE, e)
+                late_s.append((i, c0, n, ps, ev([PE.matmul(ps[:, 0:n], T.one[:], T.xs[:, c0:c0 + n], False, True)])))
+        for i, c0, n, ps, e in late_s:
+            wait(SC, e)
+            evs[i] = ev([SC.activation(T.res[:, c0:c0 + n], ps[:, 0:n], F.Copy)])
+        for i, (c0, n, who) in enumerate(CFG["fs"]):
+            wait(Q, evs[i])
+            stores.append(Q.dma_start(T.y[:, c0:c0 + n], T.res[:, c0:c0 + n]))
+    for i, n in enumerate([] if CFG["fs"] else CFG["fin"]):
         u0, u1 = c0 // 16, (c0 + n) // 16
+        if CFG["fb"] and i == CFG["fb"]:
+            e_half = whole(1) if CFG["il"] == 2 else pointer(1)
+        if CFG["fb"] and i == CFG["fb"] - 1 and CFG["il"] == 2:
+            larger(1)
+        if CFG["fb"] and c0 <= K < c0 + n:
+            wait(V, e_half)
+            wait(SC, e_half)
         if late:
             wait(V, e_fld)
             e = ev([V.tensor_tensor(T.res[:, c0:c0 + n], T.hist[:].indirect(T.ptr[:, f0 + u0:f0 + u1]), T.kind[:, c0:c0 + n], A.add)])
@@ -385,5 +596,5 @@ def rank_program(g, core, T, topo):
         stores.append(Q.dma_start(T.y[:, c0:c0 + n], T.res[:, c0:c0 + n]))
         c0 += n
     wait(Q, ev(stores, 16))
-    g.wait_ge(T.sem.sent, R * sum(s * (k1 - k0) for s, (k0, k1) in zip(share, parts)))
+    g.wait_ge(T.sem.sent, R * sum(s * (k1 - k0) for s, (k0, k1, _) in zip(share, parts)))
     wait(g, *[e for e in made if e[0] not in waited])

from concourse.bass import DstId, RemoteDMATransfer
from concourse.mybir import AluOpType as A, ActivationFunctionType as F

N, P, S, R = 8, 2048, 48, 5
K = 1024
H = K // 2
L = S * S
HIST = P + R * K
RADIX = 32
PK = L // 16

CFG = {"late": 0, "old": 0, "gf": [20, 20, 20, 20, 20], "gn": [24, 24, 24, 24, 24], "pgv": [32, 32, 32, 32], "sa": [512, 512, 512, 512, 512],
       "pg": [0, 0, 0, 0, 0], "pm": [1, 1, 1, 1, 1], "pt": [2, 2, 2, 2, 2], "wz": 256, "wv": 0, "wl": 0, "ws": 512, "cv": 512, "x0": 32,
       "fin": [256, 768, 1024], "fv": 0.5, "os": [0] * 5, "wg": 0, "b1": 1, "near": [3], "mo": [0] * 5, "mo2": [0] * 5,
       "dg": 0, "zg": 0, "sl": 0, "pk": 1, "p11": -1, "l0": 768, "th": 0, "nm": 1, "fb": 0, "fs": 0, "tr": [0, 0], "go": [1] * 5, "nk": 0, "c_idh": 4, "fl": 0, "il": 0,
       "c_sign": 0, "c_wl": 2, "c_tab": 3, "c_taba": 2, "c_dk": 3, "c_id": 4, "c_offs": 4, "c_hi": 4, "c_ed": 4, "c_lf": 4, "c_x0": 4, "tp": 5}

CFG.update({'late': 1, 'sa': [512, 512, 768, 768, 512], 'pg': [0, 0, -1, -1, 0], 'pm': [1, 1, 0, 0, 2], 'pt': [1, 2, 1, 1, 3], 'mo': [1, 0, 0, 0, 0], 'wz': 128, 'wv': 256, 'ws': 0, 'cv': 0, 'fin': [256, 384, 384, 512, 512], 'dg': 1, 'th': 1, 'fb': 2, 'c_id': 0, 'c_offs': 3, 'c_hi': 1, 'c_taba': 3, 'l0': 512})

CFG.update({'pgv': [32, 28, 28, 24], 'sa': [512, 768, 768, 768, 512], 'pg': [0, -1, -1, -1, 0], 'pm': [1, 0, 0, 0, 2], 'pt': [2, 1, 1, 1, 3], 'wz': 128, 'wv': 0, 'ws': 256, 'wg': 512, 'mo': [0] * 5, 'fb': 1, 'c_id': 4, 'c_offs': 3, 'c_hi': 0, 'c_lf': 3, 'tp': 7,
            'fs': [(0, 384, 'v'), (384, 256, 'v'), (640, 384, 's'), (1664, 384, 's'), (1024, 640, 'v')]})

CFG.update({'late': 1, 'old': 1, 'gf': [16, 16, 20, 16, 20], 'gn': [32, 32, 32, 32, 28], 'pgv': [32, 28, 24, 28], 'sa': [512, 512, 640, 512, 512], 'pg': [0, 0, 0, 0, 1], 'pm': [1, 1, 1, 1, 2], 'pt': [1, 2, 2, 2, 3], 'wz': 128, 'wv': 256, 'wl': 0, 'ws': 0, 'cv': 0, 'os': [1, 1, 1, 1, 0], 'wg': 256, 'b1': 1, 'mo': [1, 0, 0, 0, 0], 'dg': 0, 'l0': 768, 'th': 0, 'fb': 1, 'fs': [(0, 512, 'v'), (512, 512, 's'), (1024, 1024, 'v')], 'c_sign': 0, 'c_tab': 3, 'c_id': 0, 'c_offs': 4, 'c_hi': 4, 'c_ed': 4, 'c_lf': 3, 'tp': 9})

CFG.update({'late': 0, 'old': 1, 'gf': [16] * 5, 'gn': [32] * 5, 'pgv': [20, 28, 28, 28], 'sa': [512] * 5, 'pg': [0] * 5, 'pm': [1, 1, 1, 1, 2], 'pt': [1, 2, 2, 2, 3], 'wz': 128, 'wv': 512, 'wl': 0, 'ws': 0, 'cv': 0, 'fin': [512, 512, 1024], 'fv': 0.45, 'os': [1] * 5, 'wg': 256, 'b1': 1, 'mo': [1, 0, 0, 0, 0], 'dg': 0, 'l0': 0, 'th': 0, 'fb': 1, 'fs': 0, 'nk': 1, 'c_sign': 0, 'c_tab': 3, 'c_id': 3, 'c_offs': 0, 'c_hi': 4, 'c_ed': 4, 'c_lf': 1, 'tp': 7, 'xp': [0] * 5, 'il': 1})

SCRATCH = {
    "la3": ("sbuf", [128, R, 32], "int32"), "lb3": ("sbuf", [128, R, 32], "int32"),
    "lst": ("sbuf", [128, R, 64], "uint16"), "lf": ("sbuf", [128, R, 64], "float32"),
    "hist": ("sbuf", [128, HIST], "bfloat16"), "laws": ("sbuf", [128, 2 * L], "bfloat16"),
    "pk": ("sbuf", [128, 2 * PK], "bfloat16"), "was": ("sbuf", [128, PK], "bfloat16"), "dk": ("sbuf", [128, 2 * PK], "bfloat16"),
    "where": ("sbuf", [128, P], "float32"), "pos": ("sbuf", [128, (R - 1) * K + H], "float32"),
    "hi": ("sbuf", [128, 4 * RADIX], "float32"),
    "xs": ("sbuf", [128, R * K], "bfloat16"), "x0": ("sbuf", [128, K], "bfloat16"),
    "pd": ("sbuf", [128, (R - 1) * K + P], "bfloat16"),
    "ptf": ("sbuf", [128, (R - 1) * 64 + 128], "float32"), "ptr": ("sbuf", [128, (R - 1) * 64 + 128], "uint16"),
    "out": ("sbuf", [128, R * 64], "bfloat16"), "land": ("sbuf", [128, R * 64], "bfloat16"),
    "col": ("sbuf", [128, R * 64], "uint16"), "offs": ("sbuf", [128, 40], "bfloat16"),
    "pidx": ("sbuf", [128, 1], "int32"), "pm": ("sbuf", [128, 1], "int32"), "cst": ("sbuf", [128, 12], "float32"),
    "ph": ("sbuf", [128, 1], "int32"), "xt": ("sbuf", [128, K], "bfloat16"),
    "e0": ("sbuf", [128, 160], "bfloat16"), "e1": ("sbuf", [128, 160], "bfloat16"),
    "diag": ("sbuf", [128, 160], "float32"), "eb": ("sbuf", [128, 144], "bfloat16"), "ed": ("sbuf", [128, 144], "bfloat16"),
    "one": ("sbuf", [128, 128], "bfloat16"), "big": ("sbuf", [128, 128], "bfloat16"),
    "num0": ("sbuf", [128, 128], "float32"), "num": ("sbuf", [128, 128], "float32"),
    "kind": ("sbuf", [128, P], "bfloat16"), "res": ("sbuf", [128, P], "float32"),
    "psa0": ("psum", [128, 512], "float32"), "psa1": ("psum", [128, 512], "float32"),
    "psc0": ("psum", [128, 512], "float32"), "psc1": ("psum", [128, 512], "float32"),
    "psc2": ("psum", [128, 512], "float32"), "psc3": ("psum", [128, 512], "float32"),
    "psp0": ("psum", [128, 512], "float32"), "psp1": ("psum", [128, 512], "float32"),
}
SEMAPHORES = ["arr%d_%d" % (t, i) for t in range(R) for i in range(3)] + ["sent", "vv", "vp"] + ["e%d" % i for i in range(132)]


def rank_program(g, core, T, topo):
    me = T.rank_of(core)
    if me is None:
        return
    V, SC, PE, Q = g.vector, g.scalar, g.tensor, g.sync
    made, waited, steps = [], {}, [0, 0]

    def ev(calls, n=1):
        name = "e%d" % len(made)
        for c in calls:
            c.then_inc(T.sem[name], n)
        made.append((name, n * len(calls)))
        return made[-1]

    def wait(q, *events):
        for e in events:
            q.wait_ge(T.sem[e[0]], e[1])
            waited[e[0]] = 1

    def step(*calls):
        for c in calls:
            c.then_inc(T.sem.vv, 1)
        steps[0] += len(calls)
        V.wait_ge(T.sem.vv, steps[0])

    def to_list(ps, eye, src, c0, n):
        last = None
        for m in range(16):
            last = PE.matmul(ps[:, 0:n], eye[:, 16 - m:144 - m], src[:, c0 + m:c0 + 16 * n:16], m == 0, m == 15)
        return ev([last])

    def iota(out, pattern, base, mult):
        return ev([g.iota(out, pattern, base, mult, allow_small_or_imprecise_dtypes=True)])

    def shared(out, o0, win, off, u0, um, u1):
        calls = []
        if um > u0:
            calls.append(V.tensor_copy(out[:, o0:o0 + 16 * (um - u0)], win.indirect(off(u0, um))))
        if u1 > um:
            calls.append(SC.activation(out[:, o0 + 16 * (um - u0):o0 + 16 * (u1 - u0)], win.indirect(off(um, u1)), F.Copy))
        return ev(calls)

    def blocks(r):
        same = [d for d in range(N) if topo.die(T.cores[d]) == topo.die(T.cores[r])]
        i = same.index(r) + 1
        return same[i:] + same[:i] + [d for d in range(N) if d not in same]

    order = blocks(me)
    own = order.index(me)
    eng = topo.engines(core, T.cores[order[-1]])
    parts, k0 = [(own + 1, N, 0)], 0
    for n in CFG["near"]:
        parts.append((k0, k0 + n, 1))
        k0 += n
    share = [len(eng) // (1 << (k1 - k0 - 1).bit_length()) for k0, k1, _ in parts]

    late, wz, l0, xm, dl, th = CFG["late"], CFG["wz"], CFG["l0"], CFG["old"] == 1, CFG["old"] == 2, CFG["th"]
    wv = wz + CFG["wv"]
    wl = wv + CFG["wl"]
    ws = wl + CFG["ws"]
    e_la = ev([Q.dma_start(T.la3[:], T.la[:]), SC.dma_start(T.lb3[:], T.lb[:])], 16)
    tr, nk = CFG["tr"], CFG["nk"]
    if nk:
        e_sp = ev([Q.dma_start(T.hist[:, 0:P], T.fld[:])], 16)
    e_lawa = [ev([Q.dma_start(T.laws[:, 0:l0], T.law[:, 0:l0])], 16)] if l0 else []
    e_w0 = iota(T.where[:, 0:wz], [[0, wz]], 0, 0) if CFG["zg"] else ev([V.memset(T.where[:, 0:wz], 0.0)])
    first = T.hist if late or nk else T.kind
    if not nk:
        e_sp0 = ev([V.memset(first[:, 0:P], 0.0)])
        wait(Q, e_sp0)
        e_sp = ev([Q.dma_start(first[0:128:16, 0:P], T.fld[0:128:16, :])], 16)

    def law():
        pk = ev([Q.dma_start(T.pk[:, i * PK:(i + 1) * PK], T.law[i:128:16, :]) for i in range(2)], 16) if dl else None
        return pk, ev([Q.dma_start(T.laws[:, l0:L], T.law[:, l0:L])], 16)

    if CFG["pk"] == 0:
        e_pk, e_law = law()

    low = [[0, H // RADIX], [1, RADIX]]
    e_p = ev([g.iota(T.pidx[:], [[0, 1]], 0, 1)])
    if CFG["dg"]:
        e_diag = iota(T.diag[:], [[1, 160]], -16, -1)
    e_lo = [iota(T.pos[:, H:K], low, RADIX, 0)]
    if not CFG["dg"]:
        e_diag = iota(T.diag[:], [[1, 160]], -16, -1)
    wg = P - CFG["wg"]
    e_wg = [iota(T.where[:, wg:P], [[0, P - wg]], 0, 0)] if wg < P else []
    e_lo.append(iota(T.pos[:, K:K + H], low, RADIX, 0))
    if dl:
        e_was = iota(T.was[:], [[0, PK // S], [1, S]], 0, 0)

    def upper(c0, n, first):
        return iota(T.pos[:, c0:c0 + n], [[1, n // RADIX], [0, RADIX]], first // RADIX, 0)

    if CFG["b1"]:
        e_b1 = upper(0, H, P + K)
    wait(SC, e_w0)

    def zero(c0, c1):
        return ev([SC.activation(T.where[:, c:min(c1, c + wz)], T.where[:, 0:min(wz, c1 - c)], F.Silu) for c in range(c0, c1, wz)])

    e_w2 = zero(ws, wg)
    wait(V, e_p)
    step(V.tensor_scalar(T.pm[:], T.pidx[:], 15, None, A.bitwise_and))
    row0, sign, pmf, keep, neg, wt, wd, w0, w1 = (T.cst[:, i:i + 1] for i in range(9))
    step(V.tensor_copy(pmf, T.pm[:]), *[V.tensor_scalar(row0, T.pm[:], 0.0, None, A.is_equal) for _ in range(0 in tr)])
    wait(V, e_w0)

    def high(t):
        src, add = (T.hi[:, 0:RADIX], 0.0) if t else (T.where[:, 0:RADIX], pmf)
        return ev([V.tensor_scalar(T.hi[:, RADIX * j:RADIX * (j + 1)], src, add, float(16 * j + (0 if t else P // RADIX)), A.add, A.add)
                   for j in ((3,) if t else (0, 1))])

    def patch(j, c0):
        return ev([Q.dma_start(T.pos[0:128:16, c0:c0 + H], T.hi[:, RADIX * j:RADIX * (j + 1)])], 16)

    def lower(c0, n):
        return ev([Q.dma_start(T.pos[1:128:16, c0:c0 + n], T.pos[1:128:16, H:H + n])], 16)

    def eye():
        wait(V, e_diag)
        return ev([V.tensor_scalar(T.eb[:], T.diag[:, 0:144], 0.0, row0, A.is_equal, A.mult)]) if 0 in tr else None

    def tables(c0, c1):
        e = ev([V.tensor_scalar(T.laws[:, L + c0:L + c1], T.laws[:, c0:c1], sign, None, A.mult)])
        wait(Q, e)
        if dl:
            wait(Q, done["dk"])
            calls = [Q.dma_start(T.laws[0:128:16, i * L:(i + 1) * L], T.dk[:, i * PK:(i + 1) * PK]) for i in range(2)]
        else:
            calls = [Q.dma_start(T.laws[0:128:16, L + c0:L + c1], T.law[1:128:16, c0:c1])]
        return ev(calls + [Q.dma_start(T.laws[1:128:16, c0:c1], T.laws[1:128:16, L + c0:L + c1])], 16)

    e_hi = {0: high(0)}
    e_w1 = [ev([V.memset(T.where[:, wz:wv], 0.0)])] if wv > wz else []
    if CFG["dg"]:
        e_eb = eye()
    done = {}

    def chore(name):
        if name == "id":
            wait(V, e_diag)
            return ev([V.tensor_scalar(T.one[:], T.diag[:, 16:144], 0.0, None, A.is_equal)] +
                      [V.tensor_scalar(T.big[:], T.diag[:, 16:144], 0.0, float(S), A.is_equal, A.mult) for _ in range(0 in tr)])
        if name == "idh":
            wait(V, e_diag)
            step(V.tensor_scalar(T.ph[:], T.pidx[:], 16, None, A.bitwise_and))
            step(V.tensor_scalar(w0, T.ph[:], 0.0, float(S), A.is_equal, A.mult), V.tensor_scalar(w1, T.ph[:], 0.0, None, A.not_equal))
            return ev([V.tensor_scalar(T.e0[:], T.diag[:], 0.0, w0, A.is_equal, A.mult),
                       V.tensor_scalar(T.e1[:], T.diag[:], 0.0, w1, A.is_equal, A.mult)])
        if name == "offs":
            return ev([V.memset(T.offs[:, 0:40:2], 0.0), V.memset(T.offs[:, 1:40:2], float(L))])
        if name == "hi":
            wait(V, e_hi[0])
            return high(1)
        if name == "ed":
            wait(V, e_diag)
            step(V.tensor_scalar(neg, T.pm[:], -1.0, None, A.mult),
                 V.tensor_scalar(wt, T.pm[:], 1.0 - RADIX, float(RADIX), A.mult, A.add))
            step(V.tensor_scalar(wd, wt, 0.0, None, A.max))
            return ev([V.tensor_scalar(T.ed[:], T.diag[:, 0:144], neg, wd, A.is_equal, A.mult)])
        if name == "lf":
            wait(V, *e_lst)
            return ev([V.tensor_scalar(T.lf[:, 1:R, :], T.lst[:, 1:R, :], float(RADIX), None, A.add)])
        if name == "wl":
            return ev([V.memset(T.where[:, wv:wl], 0.0)])
        if name == "sign":
            more = [V.tensor_scalar(keep, T.pm[:], -float(PK // S), None, A.mult)] if dl else \
                [V.tensor_scalar(keep, T.pm[:], 0.0, None, A.not_equal)] if xm or not late else []
            return ev([V.tensor_scalar(sign, T.pm[:], 2.0, -1.0, A.is_ge, A.mult)] + more)
        if name == "dk":
            wait(V, e_pk, e_was, done["sign"])
            return ev([V.tensor_tensor(T.dk[:, PK:2 * PK], T.pk[:, PK:2 * PK], T.was[:], A.subtract)] +
                      [V.tensor_scalar(T.dk[:, i * S:(i + 1) * S], T.pk[:, i * S:(i + 1) * S], keep, -float(i), A.add, A.add)
                       for i in range(PK // S)])
        if name == "taba":
            wait(V, *e_lawa, done["sign"])
            return tables(0, l0)
        if name == "tab":
            wait(V, e_law, *e_lawa, done["sign"])
            return tables(l0 if th else 0, L)
        wait(V, e_fld, done["sign"])
        win = T.hist[:, 0:P].indirect(T.lst[:, 0, 0:CFG["x0"]])
        o = T.x0[:, 0:16 * CFG["x0"]]
        return ev([V.tensor_copy(o, win) if dl else V.tensor_scalar(o, win, keep, None, A.mult)])

    def chores(slot):
        names = ["wl", "hi", "sign", "dk", "taba", "offs", "id", "idh", "ed", "lf", "x0"]
        names.insert(CFG["tp"], "tab")
        skip = ["wl"] * (wl == wv) + ["x0"] * (late or nk) + ["dk"] * (not dl) + ["taba"] * (not th) + ["idh"] * (1 not in tr)
        for name in names:
            if CFG["c_" + name] == slot and name not in skip:
                done[name] = chore(name)

    chores(0)
    wait(Q, e_hi[0], e_lo[0])
    e_pos = {0: [patch(0, H)]}
    if CFG["pk"] == 1:
        e_pk, e_law = law()
    wait(Q, e_lo[1])
    e_pos[0].append(patch(1, K))
    pieces = []
    if not nk and not (late and CFG["fl"]):
        e_fld = ev([Q.dma_start(T.kind[:] if late else T.hist[:, 0:P], T.fld[:])], 16)
    if CFG["b1"]:
        wait(Q, e_b1)
        e_pos[1] = [lower(0, H)]

    def moves(k0, k1):
        calls = []
        while k0 < k1:
            k = k0 + 1
            while k < k1 and order[k] == order[k - 1] + 1:
                k += 1
            d0, d1 = order[k0], order[k - 1] + 1
            calls += [V.tensor_copy(T.lst[:, :, 8 * k0:8 * k:2], T.la3[:, :, 4 * d0:4 * d1]),
                      V.tensor_copy(T.lst[:, :, 8 * k0 + 1:8 * k:2], T.lb3[:, :, 4 * d0:4 * d1])]
            k0 = k
        return ev(calls)

    wait(V, e_la)
    e_lst = [moves(own + CFG["os"][0], N) if CFG["sl"] else moves(0, N)]
    if not CFG["dg"]:
        e_eb = eye()
    chores(1)

    def scatter(t, a, b):
        c0 = (t - 1) * K + H if t > 1 else H - t * H
        return ev([SC.activation(T.where[:].indirect(T.lst[:, t, a // 16:b // 16]), T.pos[:, c0 + a:c0 + b], F.Silu)])

    ready, e_sa, e_sb = [e_sp, e_lst[0]], None, None
    for t in range(R):
        b, c = t * K, t * 64
        mine = CFG["os"][t]
        spans = [(8 * (own + mine), 64), (0, 8 * (own + mine))]
        if t:
            win, off = T.hist[:, 0:P + t * K], lambda u0, u1: T.ptr[:, c - 64 + u0:c - 64 + u1]
        else:
            win, off = first[:, 0:P], lambda u0, u1: T.lst[:, 0, u0:u1]
        if 0 < t < R - 1:
            wait(Q, ready[-1], e_hi[t + 1])
            e_pos[t + 1] = [lower(t * K + H, K)] * 2
            if late and CFG["fl"]:
                c0, c1 = (t - 1) * 704, min(P, t * 704)
                pieces.append(Q.dma_start(T.kind[:, c0:c1], T.fld[:, c0:c1]))
        if late and t == (R - 1 if CFG["fl"] else 1):
            wait(Q, ev(pieces, 16) if pieces else e_fld)
            e_fld = ev([Q.dma_start(T.kind[0:128:16, :], T.hist[1:128:16, 0:P])], 16)
        wait(V, *ready)
        wait(SC, *ready)
        e_x, e_mm, e_out, e_old, jobs, ready, tail = [], [], [], [], [], [], []
        e_x, e_mm, part_x, go = {}, {}, {}, CFG["go"][t]
        e_old = [None, None] if t else []

        def forget(c0, c1):
            src = T.laws[1:128:16, L + c0:L + c1] if nk else first[1:128:16, c0:c1]
            return ev([Q.dma_start(T.xs[0:128:16, b + c0:b + c1], src)], 16)

        def masked(u0, u1):
            wait(V, *e_x.values(), done["sign"])
            return ev([V.tensor_scalar(T.x0[:, 16 * u0:16 * u1], T.xs[:, b + 16 * u0:b + 16 * u1], keep, None, A.mult)])

        def gather(i, who):
            u0, u1 = spans[i]
            um = min(u1, u0 + CFG["gn" if i else "gf"][t])
            if who and um < u1:
                part_x[i] = [SC.activation(T.xs[:, b + 16 * um:b + 16 * u1], win.indirect(off(um, u1)), F.Copy)]
            if not who:
                e_x[i] = ev(part_x.get(i, []) + [V.tensor_copy(T.xs[:, b + 16 * u0:b + 16 * um], win.indirect(off(u0, um)))])

        def listed(i):
            u0, u1 = spans[i]
            if tr[i]:
                wait(V, e_x[i])
                e_mm[i] = ev([V.transpose(T.xt[:, 16 * u0:16 * u1], T.xs[:, b + 16 * u0:b + 16 * u1])])
            else:
                wait(PE, e_x[i])
                e_mm[i] = to_list(T["psa%d" % i], T.eb, T.xs, b + 16 * u0, u1 - u0)
            if t and CFG["old"] == 0:
                wait(Q, e_mm[i])
                e_old[i] = forget(16 * u0, 16 * u1)

        if t == 0 and 0 in tr:
            wait(PE, e_eb)
        for i in ((1, 0) if go == 2 else (0, 1)):
            if t == 0 and i == 1 and CFG["sl"]:
                e_lst.append(moves(0, spans[1][1] // 8))
                wait(V, e_lst[1])
                wait(SC, e_lst[1])
            gather(i, 1)
            if go or i == 0:
                gather(i, 0)
                if not tr[i]:
                    listed(i)
        if t == 0:
            if ws > wl:
                e_w1.append(zero(wl, ws))
            chores(2)
        if dl and t:
            e_old = e_x

        sa = CFG["sa"][t]
        if t == 0:
            wait(SC, e_pos[0][0], e_w2, e_hi[0], *e_w1, *e_wg, *([done["wl"]] if wl > wv else []))
            e_sa = scatter(0, 0, sa)
        wait(SC, e_sa, *e_pos[t])
        e_sb = scatter(t, sa, K) if sa < K else e_sa

        def newest():
            if CFG["pgv"][t] if t + 1 < R else CFG["cv"]:
                wait(V, e_sb)
            wait(SC, e_sb)
            if t + 1 < R:
                e_pg = shared(T.pd, b, T.where[:], lambda u0, u1: T.lst[:, t + 1, u0:u1], 0, CFG["pgv"][t], 64)
                jobs.append((e_pg, T["psp%d" % (t % 2)], b, T.lf[:, t + 1, :], c))
                n0 = CFG["x0"]
                if t == 0 and not late and not nk and n0 < 64:
                    wait(SC, e_fld, done["sign"])
                    rest = T.x0[:, 16 * n0:K], T.hist[:, 0:P].indirect(off(n0, 64)), F.Copy
                    e_old.append(ev([SC.activation(*rest) if dl else SC.activation(*rest, scale=keep)]))
                n = CFG["sa"][t + 1]
                if n == 0:
                    return e_pg
                wait(SC, e_pg, *e_pos[t + 1][:1 + (n > H)])
                return scatter(t + 1, 0, n)
            cv = CFG["cv"]
            for u in range(2):
                a = u * K
                calls = [V.tensor_copy(T.pd[:, b + a:b + a + cv], T.where[:, a:a + cv])] if cv else []
                if cv < K:
                    calls.append(SC.activation(T.pd[:, b + a + cv:b + a + K], T.where[:, a + cv:a + K], F.Copy))
                jobs.append((ev(calls), T["psp%d" % u], b + a, T.num[:, 64 * u:64 * u + 64], c + 64 * u))
            return None

        for i, (u0, u1) in enumerate(spans):
            if t == 0 and i == 1:
                chores(3)
            if i not in e_x:
                gather(i, 0)
            if i not in e_mm:
                listed(i)
            if xm and (t or nk) and i == 1 and CFG["xp"][t] < 2:
                e_old = [masked(0, 64)] * 2 if CFG["xp"][t] == 0 else [masked(*spans[0])]
            if i == 1 and CFG["pg"][t] < 0:
                e_sa = newest()
            wait(V, e_mm[i])
            src = T.xt[:, 16 * u0:16 * u1:16] if tr[i] else T["psa%d" % i][:, 0:u1 - u0]
            e_out.append(ev([V.tensor_copy(T.out[:, c + u0:c + u1], src)]))
            wait(g, e_out[i])
            for j in [j for j, part in enumerate(parts) if part[2] == i]:
                transfers = []
                for n, k in enumerate(range(*parts[j][:2])):
                    d = order[k]
                    rid, pid, _ = topo.addr(T.cores[d])
                    at = c + 8 * blocks(d).index(me)
                    transfers.append(RemoteDMATransfer(dst_ids=[DstId(rid=rid, pnc=pid)],
                                                       dma_engine_mask=sum(1 << e for e in eng[share[j] * n:share[j] * (n + 1)]),
                                                       remote_sem=T.sem["arr%d_%d" % (t, j)], src=T.out[:, c + 8 * k:c + 8 * k + 8],
                                                       dst=T.land[:, at:at + 8]))
                g.remote_dma_fused(transfers, local_sem=T.sem.sent)
        if xm and (t or nk) and CFG["xp"][t]:
            e_old = [masked(0, 64)] * 2 if CFG["xp"][t] == 2 else e_old + [masked(*spans[1])]
        if t == 0 and not CFG["b1"]:
            e_b1 = upper(0, H, P + K)
        if t + 2 < R:
            e_hi[t + 2] = upper((t + 1) * K + H, K, P + (t + 2) * K)
        elif t + 2 == R:
            e_num0 = iota(T.num0[:], [[16, 128]], RADIX, 0)
        if t == R - 2 + CFG["nm"]:
            wait(V, e_num0)
            e_num = ev([V.tensor_scalar(T.num[:], T.num0[:], pmf, None, A.add)])

        def own_terms(ps, k0, k1, mixed):
            n, a = 8 * (k1 - k0), c + 8 * k0
            PE.matmul(ps[:, 0:n], T.one[:], T.offs[:, 0:n], True, False)
            if mixed:
                for y in range(2):
                    PE.matmul(ps[:, 0:n:2], T.e0[:, 16 - 16 * y:144 - 16 * y], T.out[:, a + y:a + n:2], False, False)
                    PE.matmul(ps[:, 1:n:2], T.e1[:, 32 - 16 * y:160 - 16 * y], T.out[:, a + y:a + n:2], False, False)
                return
            PE.matmul(ps[:, 0:n:2], T.big[:], T.out[:, a:a + n:2], False, False)
            PE.matmul(ps[:, 1:n:2], T.one[:], T.out[:, a + 1:a + n:2], False, False)

        def partner_terms(ps, o, src, k0, k1, last, mixed):
            n, a = 8 * (k1 - k0), c + 8 * k0
            if mixed:
                for y in range(2):
                    PE.matmul(ps[:, o:o + n:2], T.e1[:, 32 - 16 * y:160 - 16 * y], src[:, a + y:a + n:2], False, False)
                    call = PE.matmul(ps[:, o + 1:o + n:2], T.e0[:, 16 - 16 * y:144 - 16 * y], src[:, a + y:a + n:2], False, last and y == 1)
                return ev([call]) if last else None
            PE.matmul(ps[:, o:o + n:2], T.one[:], src[:, a + 1:a + n:2], False, False)
            call = PE.matmul(ps[:, o + 1:o + n:2], T.big[:], src[:, a:a + n:2], False, last)
            return ev([call]) if last else None

        looks = [(k0, k1, j, span) for j, (k0, k1, span) in enumerate(parts)]
        if CFG["mo"][t]:
            looks = [(min(k0, own), max(k1, own + 1), j, span) if span == mine and (k1 == own or k0 == own + 1) else (k0, k1, j, span)
                     for k0, k1, j, span in looks]
        else:
            looks.insert(CFG["mo2"][t], (own, own + 1, None, mine))

        if t == 0:
            chores(4)
            wait(Q, done["hi"], e_sa)
            e_second = patch(3, H)
            if not CFG["b1"]:
                wait(Q, e_b1)
                e_pos[1] = [lower(0, H)]
            e_pos[1].append(e_second)
            wait(PE, *[done[n] for n in ("id", "offs", "idh") if n in done])
            if nk and CFG["old"] == 0:
                wait(Q, *e_mm.values())
                done["x0"] = forget(0, K)
            e_old = e_old + [done[n] for n in ("tab", "taba", "x0") if n in done]
        e_sum = {}
        for i, (k0, k1, j, span) in sorted(enumerate(looks), key=lambda x: (x[1][3], x[1][2] is not None)):
            wait(PE, e_out[span])
            own_terms(T["psc%d" % i], k0, k1, tr[span])
            if k0 <= own < k1:
                e_sum[i] = partner_terms(T["psc%d" % i], 8 * (own - k0), T.out, own, own + 1, j is None, tr[span])

        todo = [i for i, x in enumerate(looks) if x[2] is not None]
        todo.insert(min(CFG["pm"][t], len(parts)), "list")

        def tensor_until(item):
            while item in todo:
                j = todo.pop(0)
                if j == "list":
                    if t == 0:
                        wait(PE, done["ed"])
                    for e, ps, c0, _, _ in jobs:
                        wait(PE, e)
                        tail.append(to_list(ps, T.ed, T.pd, c0, 64))
                else:
                    k0, _, r, _ = looks[j]
                    PE.wait_ge(T.sem["arr%d_%d" % (t, r)], share[r] * (parts[r][1] - parts[r][0]))
                    e_sum[j] = partner_terms(T["psc%d" % j], 8 * (parts[r][0] - k0), T.land, parts[r][0], parts[r][1], True, tr[parts[r][2]])

        def larger(u):
            _, ps, _, like, c0 = jobs[u]
            wait(V, tail[u])
            V.tensor_tensor(T.ptf[:, c0:c0 + 64], ps[:, 0:64], like, A.max).then_inc(T.sem.vp, 1)
            steps[1] += 1

        def whole(u):
            c0 = jobs[u][4]
            V.wait_ge(T.sem.vp, steps[1])
            return ev([V.tensor_scalar(T.ptr[:, c0:c0 + 64], T.ptf[:, c0:c0 + 64], 0.25 - RADIX, None, A.add)])

        def pointer(u):
            larger(u)
            return whole(u)

        news = []
        for i, (k0, k1, j, span) in enumerate(looks + [(0, 0, 0, 0)]):
            if i == min(CFG["pg"][t], len(looks)):
                e_sa = newest()
            now = i == min(CFG["pt"][t], len(looks))
            if now:
                tensor_until("list")
                if t == 0:
                    wait(V, done["lf"])
                if t + 1 == R:
                    wait(V, e_num)
                if t + 1 == R and not CFG["fb"]:
                    ready.append(pointer(1))
                larger(0)
            if k1 == 0 or not CFG["il"]:
                if now:
                    ready.append(whole(0))
                now = False
            if k1 == 0:
                break
            tensor_until(i)
            u0, u1 = 8 * k0, 8 * k1
            wait(V, e_sum[i])
            V.tensor_copy(T.col[:, c + u0:c + u1], T["psc%d" % i][:, 0:u1 - u0]).then_inc(T.sem.vv, 1)
            steps[0] += 1
            if now:
                ready.append(whole(0))
            V.wait_ge(T.sem.vv, steps[0])
            if t == 0 and i == 0:
                wait(V, *e_old)
            if t:
                wait(V, e_old[span])
            new, looked = T.hist[:, P + b + 16 * u0:P + b + 16 * u1], T.laws[:].indirect(T.col[:, c + u0:c + u1])
            if t == 0 and late and not dl:
                news.append(V.tensor_copy(new, looked))
            else:
                old = T.xs[:, b + 16 * u0:b + 16 * u1] if (t or late or nk) and not xm else T.x0[:, 16 * u0:16 * u1]
                news.append(V.tensor_tensor(new, looked, old, A.add))
        ready.append(ev(news))

    f0 = (R - 1) * 64
    wait(V, *ready)
    wait(SC, *ready)
    stores, c0 = [], 0
    if CFG["fs"]:
        wait(V, e_fld)
        wait(PE, e_fld)
        e_half, evs, late_s = None, {}, []
        for i, (c0, n, who) in enumerate(CFG["fs"]):
            if who == "v":
                if c0 >= K and e_half is None:
                    e_half = pointer(1)
                    wait(V, e_half)
                evs[i] = ev([V.tensor_tensor(T.res[:, c0:c0 + n], T.hist[:].indirect(T.ptr[:, f0 + c0 // 16:f0 + (c0 + n) // 16]),
                                             T.kind[:, c0:c0 + n], A.add)])
                if i == CFG["fb"] - 1 and e_half is None:
                    e_half = pointer(1)
                    wait(V, e_half)
        for i, (c0, n, who) in enumerate(CFG["fs"]):
            if who == "s":
                if c0 >= K:
                    wait(SC, e_half)
                ps = T["psa%d" % (len(late_s) % 2)]
                e = ev([SC.activation(T.xs[:, c0:c0 + n], T.hist[:].indirect(T.ptr[:, f0 + c0 // 16:f0 + (c0 + n) // 16]), F.Copy)])
                PE.matmul(ps[:, 0:n], T.one[:], T.kind[:, c0:c0 + n], True, False)
                wait(PE, e)
                late_s.append((i, c0, n, ps, ev([PE.matmul(ps[:, 0:n], T.one[:], T.xs[:, c0:c0 + n], False, True)])))
        for i, c0, n, ps, e in late_s:
            wait(SC, e)
            evs[i] = ev([SC.activation(T.res[:, c0:c0 + n], ps[:, 0:n], F.Copy)])
        for i, (c0, n, who) in enumerate(CFG["fs"]):
            wait(Q, evs[i])
            stores.append(Q.dma_start(T.y[:, c0:c0 + n], T.res[:, c0:c0 + n]))
    for i, n in enumerate([] if CFG["fs"] else CFG["fin"]):
        u0, u1 = c0 // 16, (c0 + n) // 16
        if CFG["fb"] and i == CFG["fb"]:
            e_half = whole(1) if CFG["il"] == 2 else pointer(1)
        if CFG["fb"] and i == CFG["fb"] - 1 and CFG["il"] == 2:
            larger(1)
        if CFG["fb"] and c0 <= K < c0 + n:
            wait(V, e_half)
            wait(SC, e_half)
        if late:
            wait(V, e_fld)
            e = ev([V.tensor_tensor(T.res[:, c0:c0 + n], T.hist[:].indirect(T.ptr[:, f0 + u0:f0 + u1]), T.kind[:, c0:c0 + n], A.add)])
        else:
            e = shared(T.res, c0, T.hist[:], lambda a, b: T.ptr[:, f0 + a:f0 + b], u0, u0 + 2 * int((u1 - u0) * CFG["fv"] / 2), u1)
        wait(Q, e)
        stores.append(Q.dma_start(T.y[:, c0:c0 + n], T.res[:, c0:c0 + n]))
        c0 += n
    wait(Q, ev(stores, 16))
    g.wait_ge(T.sem.sent, R * sum(s * (k1 - k0) for s, (k0, k1, _) in zip(share, parts)))
    wait(g, *[e for e in made if e[0] not in waited])
